import numpy as np, ml_dtypes
CORES = [66,74,82,90,194,202,210,218]
N = 8
BF = ml_dtypes.bfloat16
def gentries(a):
    return np.ascontiguousarray(a.reshape(8, 16, -1).transpose(0, 2, 1)).reshape(8, -1)
def gtable(e):
    e = np.asarray(e); return np.ascontiguousarray(e.reshape(8, -1, 16).transpose(0, 2, 1)).reshape(128, -1).astype(np.int32)
V, SH, L, RO, WT = 1280, 1, 192, 4, 3
R = V << SH
NC = 8
def near(rng, X, x):
    return np.clip(np.take_along_axis(X, x[:, :, None, :], 3) + rng.integers(-1, 2, (N, 8, 16, L)), 0, 15)
def scene(rng, strong):
    M = V // NC
    lab = rng.permuted(np.tile(np.arange(V) % NC, (8, 1)), axis=1); order = np.argsort(lab, axis=1, kind="stable")
    if strong: cen = np.tile(2 + 11 * (np.arange(NC) % 2), (8, 16, 1)); w = 1
    else: cen = rng.integers(2, 14, (8, 16, NC)); w = 3
    X = np.clip(np.take_along_axis(cen, np.repeat(lab, 2 ** SH, axis=1)[:, None, :], 2)[None] + rng.integers(-w, w + 1, (N, 8, 16, R)), 0, 15)
    to = np.where(rng.random((N, 8, 16, V)) < 0.4, rng.integers(0, NC, (N, 8, 16, V)), lab[None, :, None, :])
    gene = order[np.arange(8)[None, :, None, None], to * M + rng.integers(0, M, (N, 8, 16, V))]
    P = gene * 2 ** SH + rng.integers(0, 2 ** SH, (N, 8, 16, V))
    x = rng.integers(0, R, (N, 8, L)); th = rng.integers(0, 21, (N, 8, 16, RO))
    return lab, X, P, x, near(rng, X, x), th
def pack(X, P, x, z, th):
    return {"prof": X.reshape(N, 128, R).astype(np.float32).astype(BF), "par": np.ascontiguousarray(P.reshape(N, 128, V)).astype(np.int32),
            "rec": np.stack([gtable(a) for a in x]), "zf": z.reshape(N, 128, L).astype(np.float32).astype(BF), "th": np.ascontiguousarray(th.reshape(N, 128, RO)).astype(np.int32)}
def setup_inputs(rng):
    lab, X, P, x, z, th = scene(rng, False)
    return pack(X, P, x, z, th)
def setup_inputs_spread(rng):
    X = (rng.random((N, 8, 16, R)) * 2.0 ** rng.integers(0, 5, (N, 8, 1, R))).astype(np.int64)
    P = (R * rng.random((N, 8, 16, V)) ** rng.choice(np.array([1, 1, 3]), (N, 8, 1, V))).astype(np.int64)
    x = (R * rng.random((N, 8, L)) ** rng.choice(np.array([1, 2, 4]), (N, 8, 1))).astype(np.int64)
    z = (rng.random((N, 8, 16, L)) * 2.0 ** rng.integers(0, 5, (N, 8, 1, L))).astype(np.int64)
    th = (64 * rng.random((N, 8, 16, RO)) ** 5).astype(np.int64)
    return pack(np.minimum(X, 15), np.minimum(P, R - 1), np.minimum(x, R - 1), np.minimum(z, 15), np.minimum(th, 63))
def setup_inputs_ends(rng):
    f = rng.integers(0, 2, 8); cls = rng.integers(0, 2, (8, V)); cls[:, 0] = f; cls[:, V - 1] = 1 - f
    cr = np.repeat(cls, 2 ** SH, axis=1); pure = rng.random((8, R)) < 0.75; pure[:, 0] = True; pure[:, R - 1] = True
    X = np.where(pure[None, :, None, :], 15 * cr[None, :, None, :], 15 * rng.integers(0, 2, (N, 8, 16, R)))
    own = np.where(cls == f[:, None], 0, R - 1)[None, :, None, :]; e = rng.random((N, 8, 16, V))
    P = np.where(e < 0.45, own, np.where(e < 0.65, R - 1 - own, rng.integers(0, R, (N, 8, 16, V))))
    e = rng.random((N, 8, L)); x = np.where(e < 0.35, 0, np.where(e < 0.7, R - 1, rng.integers(0, R, (N, 8, L))))
    x[:, :, 0] = 0; x[:, :, 1] = R - 1; x[:, :, L - 2] = R - 1; x[:, :, L - 1] = 0
    c = cr[np.arange(8)[None, :, None], x]; like = rng.random((N, 8, L)) < 0.8; like[:, :, :2] = True; like[:, :, L - 2:] = True
    z = np.where(like[:, :, None, :], 15 * c[:, :, None, :], 15 * rng.integers(0, 2, (N, 8, 16, L)))
    th = 63 * rng.integers(0, 2, (N, 8, 16, RO)); turn = rng.integers(0, 2, (N, 8)); turn[N - 1, 7] = 0
    for g in range(8):
        lo = np.flatnonzero(pure[g] & (cr[g] == f[g])); hi = np.flatnonzero(pure[g] & (cr[g] != f[g]))
        for q in range(N):
            a = np.where(rng.random(16) < 0.5, 0, rng.choice(lo, 16)); b = np.where(rng.random(16) < 0.5, R - 1, rng.choice(hi, 16))
            a[:2] = R - 1
            if turn[q, g]: b[15] = 0; b[1] = 0
            P[q, g, :, 0] = a; P[q, g, :, V - 1] = b
    return pack(X, P, x, z, th)
def level(rng, m):
    sh = rng.integers(0, 16, m.shape)
    return (m >> 4)[None] + (((np.arange(16)[:, None] + sh[None]) & 15) < (m & 15)[None])
def setup_inputs_corners(rng):
    lab, X, P, x, z, th = scene(rng, False)
    th[..., 0] = rng.choice(np.array([0, 0, 1, 5, 20, 63]), (N, 8, 16)); k = np.arange(16)[:, None]; l = np.arange(L)
    half = (l & 7) == 3; farx = (l & 7) == 5; fary = (l & 7) == 6; few = farx | fary; hl = np.flatnonzero(half)
    for q in range(N):
        for g in range(8):
            o = 1 + rng.permutation(V - 2); u, v, w = np.array(o[:L]), o[L:2 * L], o[2 * L:3 * L]; u[0] = 0; u[L - 1] = V - 1
            pool = rng.permutation(((o[3 * L:] << SH)[:, None] + np.arange(2 ** SH)[None]).reshape(-1))[:482]
            xr, yr, br = [(a << SH) + rng.integers(0, 2 ** SH, L) for a in (u, v, w)]; xr[0] = 0; xr[L - 1] = R - 1
            flip = rng.integers(0, 2, L); beta = rng.integers(80, 240, L); beta[hl] = 240; bm = np.where(flip == 1, 240 - beta, beta)
            X[q, g][:, pool] = level(rng, np.arange(482) % 241); X[q, g][:, yr] = (15 * (1 - flip))[None]; X[q, g][:, br] = level(rng, bm)
            rho = xr & 15; key = rng.random((16, L)); key[rho, l] = 2.0; place = np.argsort(np.argsort(key, axis=0), axis=0)
            nw = np.where(half | few, 15, rng.choice(np.array([0, WT - 1, WT, WT, WT + 1, 15]), L))
            twin = (nw == WT - 1) & (rng.random(L) < 0.25)
            X[q, g][:, yr[twin] ^ 1] = (15 * (1 - flip[twin]))[None]; th[q, g, rho[twin], 0] = 0
            e = np.where(place < nw[None], rng.choice(np.array([0, 0, 1, 5]), (16, L)), -1)
            m = beta[None] - th[q, g, :, :1] - e
            A = pool[np.where(flip[None] == 1, 240 - m, m)]
            odd = (rng.integers(0, 2, L) == 1) & ~(half | few)
            B = np.where(odd[None] & ((k & 1) == 1), pool[241 + bm][None], br[None])
            B[rho[twin], l[twin]] = yr[twin] ^ 1
            A = np.where((place == 14) & (nw[None] < 15), B, A); A[rho, l] = yr
            lo = np.where(rho == 0, 1, 0)[hl]; hi = np.where(rho == 15, 14, 15)[hl]
            A[lo, hl] = pool[np.where(flip[hl] == 1, 239, 1)]; A[hi, hl] = pool[240 * flip[hl]]; B[lo, hl] = pool[241 + bm[hl]]
            mode = rng.integers(0, 5, L)[None]; some = rng.choice(pool, (16, L))
            C = np.where(mode == 0, yr[None], np.where(mode == 1, xr[None], np.where(mode == 2, np.where(k == 15, some, yr[None]), np.where(mode == 3, np.where(rng.random((16, L)) < 0.5, yr[None], xr[None]), some))))
            far = pool[240 * np.where(farx, flip, 1 - flip)[None] + 241 * rng.integers(0, 2, (16, L))]; far[0] = np.where(farx, xr, yr)
            C = np.where(few[None], far, C)
            P[q, g][:, u] = A; P[q, g][:, v] = B; P[q, g][:, w] = C
            x[q, g] = xr; z[q, g] = (15 * flip)[None]
    return pack(X, P, x, z, th)
def setup_inputs_crowd(rng):
    lab, X, P, x, z, th = scene(rng, True); th = rng.integers(0, 64, th.shape)
    for q in range(N):
        for g in range(8):
            c = int(rng.integers(0, 2)); a = rng.permutation(np.flatnonzero((lab[g] & 1) == c)); b = rng.permutation(np.flatnonzero((lab[g] & 1) != c))
            x0 = (a[:4] << SH) + rng.integers(0, 2 ** SH, 4); y0 = (b[:4] << SH) + rng.integers(0, 2 ** SH, 4)
            for i in range(4):
                P[q, g, :, a[i]] = (rng.choice(a, 16) << SH) + rng.integers(0, 2 ** SH, 16)
                P[q, g, ((a[i] << SH) + np.arange(2 ** SH)) & 15, a[i]] = y0[i]
                P[q, g, :, b[i]] = (rng.choice(b, 16) << SH) + rng.integers(0, 2 ** SH, 16)
            mode = (g + q) % 3
            if mode == 0: x[q, g] = x0[0]
            elif mode == 1: x[q, g] = x0[rng.integers(0, 4, L)]
            else: x[q, g] = (a[0] << SH) + rng.integers(0, 2 ** SH, L)
            if q % 4 == 1 and g % 2 == 1:
                r = (a[4] << SH) + int(rng.integers(0, 2 ** SH)); P[q, g, :, a[4]] = r; x[q, g, int(rng.integers(0, L))] = r
    z = near(rng, X, x)
    for q in range(3, N, 4):
        away = rng.random((8, L)) < 0.5; away[:, 0] = True; away[:, L - 1] = False
        z[q] = np.where(away[:, None, :], 15 - z[q], z[q])
    return pack(X, P, x, z, th)
def setup_inputs_counts(rng):
    cls = rng.permuted(np.tile(np.arange(V) & 1, (8, 1)), axis=1); order = np.argsort(cls, axis=1, kind="stable")
    X = 6 + 2 * np.repeat(cls, 2 ** SH, axis=1)[None, :, None, :] + rng.integers(0, 2, (N, 8, 16, R))
    off = ((np.arange(16)[:, None] - (np.arange(V) << SH)[None]) & 15) < 2 ** SH + 2
    to = np.where(off[None, None], 1 - cls[None, :, None, :], cls[None, :, None, :])
    gene = order[np.arange(8)[None, :, None, None], to * (V // 2) + rng.integers(0, V // 2, (N, 8, 16, V))]
    P = gene * 2 ** SH + rng.integers(0, 2 ** SH, (N, 8, 16, V))
    x = rng.integers(0, R - 2 ** SH, (N, 8, L))
    for q in range(1, N, 2):
        g = int(rng.integers(0, 8)); r = ((V - 1) << SH) + int(rng.integers(0, 2 ** SH))
        P[q, g, :, V - 1] = r; x[q, g, int(rng.integers(0, L))] = r
    z = 6 + 2 * cls[np.arange(8)[None, :, None], x >> SH][:, :, None, :] + rng.integers(0, 2, (N, 8, 16, L))
    lev = 4 + 4 * rng.permuted(np.tile(np.arange(8), (N, RO, 1)), axis=2)
    th = lev.transpose(0, 2, 1)[:, :, None, :] + rng.integers(0, 4, (N, 8, 16, RO))
    th[..., 0] = 0; th[1::4, :, :, 1] = 63; th[2::4, :, :, 2] = 63; th[3::4, :, :, 2] = 63
    for q in range(1, N, 4):
        g = int(rng.integers(0, 8)); X[q, g] = 6 + rng.integers(0, 4, (16, 1))
        th[q, g, :, 2] = 63; th[q, g, rng.permutation(16)[:WT], 2] = 0
    return pack(X, P, x, z, th)
def check_inputs(d):
    bad = []
    for k, lo, hi in (("prof", 0, 15), ("par", 0, R - 1), ("rec", 0, R - 1), ("zf", 0, 15), ("th", 0, 63)):
        a = np.asarray(d[k]).astype(np.float64)
        if not (np.min(a) >= lo and np.max(a) <= hi): bad.append("range of " + k)
        elif np.any(a != np.floor(a)): bad.append("whole numbers in " + k)
    return bad
def look(tab, n):
    return np.take_along_axis(tab, n[:, None, :], 2)
def row_of(tile, k):
    return np.take_along_axis(tile, k[:, None, :], 1)[:, 0]
def dist(w, p):
    return np.add.reduce(np.abs(w - p[:, :, None, :]), axis=1)
def reference(prof, par, rec, zf, th):
    X = prof.astype(np.float32).astype(np.int32).reshape(N, 8, 16, R); P = par.astype(np.int64).reshape(N, 8, 16, V)
    x = np.stack([gentries(a) for a in rec]).astype(np.int64); z = zf.astype(np.float32).astype(np.int32).reshape(N, 8, 16, L)
    tt = th.astype(np.int64).reshape(N, 8, 16, RO); breaks = [0] * N; rows = np.arange(16)[None, :, None]
    for t in range(RO):
        for q in range(N):
            h = (q - t) % N; xs, zs = x[h], z[h]
            A = look(P[q], xs >> SH); rho = (xs + t) & 15; y = row_of(A, rho); B = look(P[q], y >> SH); Xy = look(X[q], y)
            wa = look(X[q], A.reshape(8, -1)).reshape(8, 16, 16, L); wb = look(X[q], B.reshape(8, -1)).reshape(8, 16, 16, L)
            e1 = dist(wb, zs) - dist(wa, zs); e2 = dist(wa, Xy) - dist(wb, Xy)
            s = tt[q, :, :, t][:, :, None] + (breaks[q] & 15)
            wit = (rows != rho[:, None, :]) & (A != B) & (e1 >= s) & (e2 >= s)
            broken = np.count_nonzero(wit, axis=1) >= WT
            kb = np.argmax(np.where(wit, e1 + e2, -1), axis=1)
            C = look(P[q], row_of(B, kb) >> SH); wc = look(X[q], C.reshape(8, -1)).reshape(8, 16, 16, L)
            y1 = row_of(C, np.argmin(np.where(C == y[:, None, :], 1000, dist(wc, zs)), axis=1))
            x1 = row_of(C, np.argmin(np.where(C == xs[:, None, :], 1000, dist(wc, Xy)), axis=1))
            for g in range(8):
                b = np.flatnonzero(broken[g])
                for a, new in ((xs, y1), (y, x1)):
                    u, i = np.unique(a[g, b] >> SH, return_index=True); P[q, g, rho[g, b[i]], u] = new[g, b[i]]
            breaks[q] = int(np.count_nonzero(broken))
            z[h] = np.where(broken[:, None, :], (zs + look(X[q], y1)) >> 1, zs); x[h] = np.where(broken, y1, y)
    return {"ypar": P.reshape(N, 128, V).astype(np.float32), "yrec": np.stack([gtable(a) for a in x]).astype(np.float32), "yz": z.reshape(N, 128, L).astype(np.float32).astype(BF)}

@@ -1,0 +1,671 @@
+from concourse.mybir import AluOpType as ALU, AxisListType as AX, ActivationFunctionType as AF
+
+V, R, L, RO = 1280, 2560, 192, 4
+H = 96
+BIG = float(2 ** 26)
+K16 = 65536.0
+C23 = 1.5 * 2 ** 23
+MID = 1280.0
+RND = 1.5 * 2 ** 35
+RAB = [("m", "m"), ("m", "m")]
+RC = [("m", "a"), ("a", "m")]
+GE = "aaaaaaavaaavaaavaa"
+FA = "001"
+ZA, WA_ = 1, 1
+
+F, B, I, U = "float32", "bfloat16", "int32", "uint16"
+SB = {
+    "XZ": (R + L, B), "Pi": (V, I), "Pf": (V + L, F), "thi": (4, I), "thf": (4, F), "reci": (12, I),
+    "xtab": (R + 4, F), "RM": (2576, B),
+    "pi": (4, I), "pf": (8, F), "ioA": (512, F), "ioB": (128, F), "ioC": (96, F), "ioD": (136, F), "ioE": (136, F),
+    "ioF": (136, F), "E": (512, B), "BOf": (128, F), "If": (128, F), "nIf": (128, F), "I2": (256, B), "nIb": (128, B), "penI": (128, B),
+    "brI": (128, B), "ones": (128, B), "ND": (192, B), "RSn": (192, F), "RS17": (272, F), "R01": (128, B), "I17": (136, F),
+    "Q17": (136, B), "B17": (136, B), "crow": (272, B), "W": (24 * 16, B), "Wc": (24, B), "nbI": (128, B),
+    "Wd": (128, B), "Wo": (128, B), "pw": (48, F), "DM": (24, F), "CL": (24, F), "ExY": (128, F), "ExX": (128, F), "TH": (384, B),
+    "LU": (RO * 64, U), "SU": (RO * 64, U), "ZL": ((RO + 1) * L, B), "ZS": (RO * L, B), "XF": (16, F), "XL": (16, F),
+    "Au": (L, U), "Bu": (L, U), "Cu": (L, U), "Af": (L, F), "Bf": (L, F), "Cf": (L, F), "M": (L, F), "rm": (L, B), "nrm": (L, F),
+    "rmf": (L, F), "xy": (2 * L, F), "gxy": (2 * L, F), "ys": (L, F), "p": (L, B), "zpT": (512, B), "eqab": (L, B), "eqc": (2 * L, B),
+    "WA": (16 * L, B), "WB": (16 * L, B), "WC": (16 * L, B), "MZA": (16 * L, B), "MZB": (16 * L, B), "MPA": (16 * L, B),
+    "MPB": (16 * L, B), "MZC": (16 * L, B), "DPC": (16 * L, B),
+    "G": (512, B), "w": (256, B), "key": (256, F), "wit": (256, B), "ks": (256, F), "cs": (256, B), "nbL": (16, B),
+    "kf": (16, F), "vT": (L, F), "vs": (L, F), "gC": (16, U), "nb4": (16, F), "gf": (32, F), "s": (32, F),
+    "nbl": (16, F), "ds": (2 * L, F), "t1": (32, F), "t2": (32, F), "t3": (32, F), "off": (32, U),
+    "ks2": (544, F), "yf": (32, F), "vT2": (L, F), "Ym": (L, F), "Xm": (L, F), "B1": (L, F),
+    "xs": (L, F), "wof": (16, F), "wou": (16, U), "zs": (L, F), "zr": (L, B), "zw": (L, B), "ga": (256, F), "gm": (256, F),
+    "cn": (4, F), "ci": (4, I), "ngs": (4, F),
+}
+BANKS = ["bank%d" % i for i in range(8)]
+SCRATCH = {n: ("sbuf", [128, w], d) for n, (w, d) in SB.items()}
+SCRATCH["EE"] = ("sbuf", [128, 24, 112], B)
+SB["EE"] = (24 * 112, B)
+for _b in BANKS:
+    SCRATCH[_b] = ("psum", [128, 512], F)
+ARR = ["a%s%d%d" % (k, t, c) for k in "xz" for t in range(1, RO + 1) for c in range(2)]
+DMAS = ["d%d" % i for i in range(12)]
+SEMAPHORES = ["cv", "ca", "cp", "cg", "sent"] + ARR + DMAS
+
+CY, PC, GA, SC, HOP = 0.83 * 1.2, 0.42 * 1.2, 1.56, 3.8, 80.0
+GRAIN, BIAS = 20.0, 3000.0
+CAP = {"r": 5, "k": 2, "m": 8}
+PRI = ("t30-3 ga0+1 w0-3 G0+1 WA0+1 Au0-6 WB1+6 ds1+6 zr1-6 Xm1-6 t10+9 yf0+9 TH1-1 SU0+6 SU1-6 zw1+6 gC1+6 LU0-3 EE0-1 wo1+3 ke0+3 "
+       "Cu1+6 ZS0+3 Bf1+3 yf1+9 nb1-1 rm1+9 MP1-1 DP1-3 vs1+1 Pf1+6 Ym1-1 zr0-3 wi1-1 Au1-3 nr1-3 ds0+6 of0-6 vs0-6 zs1-1 gf0+3 WA1-1 "
+       "Ym0-1 nb0-6 xy0+9 wi0-6 MZ1-6 ks0-6 gm1-1 eq0+6 vT1+3 Bu1-3 kf0+3 xy1+9 rm0-1 zp0+1 xs0+6 XZ1+6 Cf1+1 EE1+1 ga1-6 gf1-6 Bf0+3 "
+       "ke1+6 ys1+6 cs1+9 t20-3 gC0+3 zw0+6 M1+6 cs0+3 PZ1-1 Xm0-6 ks1+9 PB0-1 eq1+9 Po1-3 t31+3 Py0+1 gx0+9 w1-3 wo0-1 DP0+6 Pz0+9 "
+       "XZ0-3 Pp0+6 of1+9 B11+3 G1+6 Pk0-1 Pn0-1")
+
+
+def rank_program(g, core, T, topo):
+    rank = T.rank_of(core)
+    if rank is None:
+        return
+    n_r = len(T.cores)
+    Q = {"v": g.vector, "a": g.scalar, "p": g.tensor, "g": g, "s": g.sync}
+    ops = []
+    occ = {}
+    acc = {}
+    lazy, soft, users, cur, nt, nd, sent = [], [], {}, [0], [0], [0], [0]
+
+    def A(n, c0=0, c1=None, st=1, p=128):
+        if n[0] == "#":
+            c1 = 512 if c1 is None else c1
+            a = [None, n, c0, c1, len(range(c0, c1, st)), st, p]
+            lazy.append(a)
+            return a
+        c1 = SB[n][0] if c1 is None else c1
+        ap = T[n][0:p, c0:c1:st] if st > 1 else T[n][0:p, c0:c1]
+        return (ap, n, c0, c1, len(range(c0, c1, st)))
+
+    def P(n, p0, p1, c0, c1):
+        return (T[n][p0:p1, c0:c1], n, c0, c1, c1 - c0)
+
+    def tile(kind):
+        nt[0] += 1
+        return "#%s%d" % (kind, nt[0])
+
+    def add(e, cost, rd, wr, fn, kind="c", lat=0.0, sem=None, cnt=0, tag=""):
+        me = len(ops)
+        deps = {}
+        for a, isw in [(a, False) for a in rd] + [(a, True) for a in wr]:
+            n, c0, c1 = a[1], a[2], a[3]
+            ps = n[0] == "#"
+            if ps:
+                users.setdefault(n, [])
+                if me not in users[n]:
+                    users[n].append(me)
+                c0, c1 = 0, 512
+            keep = []
+            for (o, d0, d1, w) in acc.get(n, []):
+                hit = o != me and d0 < c1 and c0 < d1
+                same = hit and ops[o][0] == e and ops[o][5] == "c" and kind == "c"
+                if hit and (w or isw or (ps and not same)):
+                    deps[o] = deps.get(o, False) or not (same and e == "p")
+                if not (hit and (isw or ps) and c0 <= d0 and d1 <= c1 and (isw or not (w or same))):
+                    keep.append((o, d0, d1, w))
+            keep.append((me, c0, c1, isw))
+            acc[n] = keep
+        nm = ("P" + rd[0][1] if e == "p" else wr[0][1] if wr else "S") + str(cur[0])
+        occ[nm] = occ.get(nm, 0) + 1
+        ops.append([e, cost, lat, fn, deps, kind, sem, cnt, nm + "abcdefghijklmnopqrstuvwxyz"[min(occ[nm] - 1, 25)], cur[0], tag])
+        return me
+
+    def two(*xs):
+        return all(x[1][0] != "#" and SB[x[1]][1] in (B, U) for x in xs)
+
+    def vcost(n, f=1.0):
+        return max(64.0, n * f) * CY + 20
+
+    def ts(o, i, s1, s2, o0, o1=None):
+        rd = [i] + [s for s in (s1, s2) if isinstance(s, tuple)]
+        a1 = s1[0] if isinstance(s1, tuple) else s1
+        a2 = s2[0] if isinstance(s2, tuple) else s2
+        if o1 is None:
+            fn = lambda q: q.tensor_scalar(o[0], i[0], a1, None, o0)
+        else:
+            fn = lambda q: q.tensor_scalar(o[0], i[0], a1, a2, o0, o1)
+        add("v", vcost(o[4], 0.5 if two(o, i) else 1), rd, [o], fn)
+
+    def cp(o, i):
+        add("v", vcost(o[4], 0.5 if two(o, i) else 1), [i], [o], lambda q: q.tensor_copy(o[0], i[0]))
+
+    def ms(o, val):
+        add("v", vcost(o[4], 0.5 if two(o) else 1), [], [o], lambda q: q.memset(o[0], val))
+
+    def tt(o, a, b, op):
+        f = 1 if "#" in (a[1][0], b[1][0]) else 2
+        add("v", vcost(o[4], f), [a, b], [o], lambda q: q.tensor_tensor(o[0], a[0], b[0], op))
+
+    def scan(o, d0, d1, init, o0, o1):
+        add("v", vcost(o[4], 0.5 if two(o, d0, d1) else 1), [d0, d1], [o],
+            lambda q: q.tensor_tensor_scan(o[0], d0[0], d1[0], init, o0, o1))
+
+    def total(o, i):
+        add("v", 80.0, [i], [o], lambda q: q.tensor_reduce(o[0], i[0], AX.X, ALU.add))
+
+    def vg(o, win, off, b=None, op=None):
+        if b is None:
+            fn = lambda q: q.tensor_copy(o[0], win[0].indirect(off[0]))
+        else:
+            fn = lambda q: q.tensor_tensor(o[0], win[0].indirect(off[0]), b[0], op)
+        return add("v", 50 + o[4] * GA * CY, [win, off] + ([b] if b else []), [o], fn, tag="g")
+
+    def vscat(win, off, a, b):
+        add("v", 50 + a[4] * SC * CY, [off, a, b], [win],
+            lambda q: q.tensor_tensor(win[0].indirect(off[0]), a[0], b[0], ALU.add), tag="s")
+
+    def act(o, i, f=AF.Identity, bias=0.0, scale=1.0):
+        rd = [i] + [s for s in (bias, scale) if isinstance(s, tuple)]
+        bb = bias[0] if isinstance(bias, tuple) else bias
+        ss = scale[0] if isinstance(scale, tuple) else scale
+        add("a", max(64, o[4]) * CY + 40, rd, [o], lambda q: q.activation(o[0], i[0], f, bias=bb, scale=ss))
+
+    def ag(o, win, off, bias=0.0):
+        return add("a", 65 + o[4] * GA * CY, [win, off], [o],
+                   lambda q: q.activation(o[0], win[0].indirect(off[0]), AF.Identity, bias=bias), tag="g")
+
+    def mm(lst):
+        cost = 0.0
+        rd = {}
+        for (o, l, r, st, sp) in lst:
+            cost += max(min(64, l[4]), r[4]) * (4 if SB[l[1]][1] == F else 1) * PC
+            for x in (l, r):
+                rd[(x[1], x[2], x[3])] = x
+
+        def fn(q):
+            ins = None
+            for (o, l, r, st, sp) in lst:
+                ins = q.matmul(o[0], l[0], r[0], st, sp)
+            return ins
+        return add("p", cost + 20, list(rd.values()), [lst[0][0]], fn)
+
+    def iota(o, pat, base, ch):
+        if SB[o[1]][1] == I:
+            fn = lambda q: q.iota(o[0], pat, base, ch)
+        else:
+            fn = lambda q: q.iota(o[0], pat, base, ch, allow_small_or_imprecise_dtypes=True)
+        add("g", 130 + 2 * o[4] * CY, [], [o], fn)
+
+    def dma(e, out, in_, rd, wr, lat):
+        sem = T.sem[DMAS[nd[0]]]
+        nd[0] += 1
+        add(e, 60.0, rd, wr, lambda q: q.dma_start(out, in_).then_inc(sem, 16), kind="d", lat=lat, sem=sem, cnt=16)
+
+    def send(dst_rank, src, land, name):
+        dst = T.cores[dst_rank % n_r]
+        rid, pid = topo.addr(dst, core)
+        mask = topo.mask(core, dst)
+        ne = len(topo.engines(core, dst))
+        sent[0] += ne
+        me = add("g", 900.0, [src], [], lambda q: q.remote_dma(land[0], src[0], T.sem[name], T.sem.sent, pid, rid, mask), kind="r")
+        o = add("x", 0.0, [], [land], None, kind="x", lat=2500.0, sem=T.sem[name], cnt=ne)
+        ops[o][4][me] = False
+
+    dma("s", T.reci[:], T.rec[:], [], [A("reci")], 2000.0)
+    dma("s", T.Pi[:], T.par[:], [], [A("Pi")], 4000.0)
+    dma("a", T.XZ[:, 0:R], T.prof[:], [], [A("XZ", 0, R)], 4000.0)
+    dma("s", T.ZL[:, 0:L], T.zf[:], [], [A("ZL", 0, L)], 2500.0)
+    dma("s", T.thi[:], T.th[:], [], [A("thi")], 2500.0)
+
+    iota(A("pi", 0, 1), [[0, 1]], 0, 1)
+    iota(A("ioC"), [[0, 6], [1, 16]], 0, 0)
+    iota(A("ioB"), [[1, 128]], 0, 0)
+    iota(A("ioA"), [[1, 32], [0, 16]], 0, 0)
+    iota(A("DM"), [[96, 2], [0, 2], [16, 6]], V, 0)
+    iota(A("ioD"), [[1, 8], [0, 17]], 0, 0)
+    iota(A("ioE"), [[0, 8], [1, 17]], 0, 0)
+    iota(A("ioF"), [[16, 8], [1, 17]], 0, 0)
+    iota(A("xtab"), [[1, R + 4]], 0, 0)
+    ts(A("pi", 1, 2), A("pi", 0, 1), 15, None, ALU.bitwise_and)
+    ts(A("pi", 2, 3), A("pi", 0, 1), 4, None, ALU.arith_shift_right)
+    ts(A("pi", 3, 4), A("pi", 0, 1), 31, None, ALU.bitwise_and)
+    cp(A("pf", 0, 4), A("pi"))
+    pc, kc, gc, p31 = A("pf", 0, 1), A("pf", 1, 2), A("pf", 2, 3), A("pf", 3, 4)
+    ts(A("pf", 4, 5), pc, -8.0, None, ALU.add)
+    ts(A("pf", 5, 6), kc, -4096.0, 16 * 4096.0 - MID, ALU.mult, ALU.add)
+    ts(A("RM", 0, 96), A("ioC"), kc, None, ALU.is_equal)
+    w0 = 96
+    while w0 < 2576:
+        n = min(w0, 2576 - w0)
+        cp(A("RM", w0, w0 + n), A("RM", 0, n))
+        w0 += n
+    for h in range(2):
+        ts(A("ND", 96 * h, 96 * h + 96), A("ioC"), kc, -float(2 ** 24), ALU.not_equal, ALU.mult)
+    ts(A("BOf"), A("ioA", 0, 128), gc, None, ALU.is_equal)
+    ts(A("If"), A("ioB"), pc, None, ALU.is_equal)
+    ts(A("E"), A("ioA"), p31, None, ALU.is_equal)
+    ms(A("RSn"), 0.0)
+    ms(A("RSn", 0, 192, 16), -BIG)
+    ms(A("RS17"), 0.0)
+    ms(A("RS17", 0, 272, 17), BIG)
+    ms(A("R01"), 1.0)
+    ms(A("R01", 0, 128, 16), 0.0)
+    ms(A("ones"), 1.0)
+    act(A("I2", 0, 128), A("If"))
+    act(A("I2", 128, 256), A("If"))
+    act(A("nIf"), A("If"), scale=-1.0)
+    act(A("nIb"), A("If"), scale=-1.0)
+    act(A("penI"), A("If"), scale=-1024.0)
+    act(A("brI"), A("If"), scale=121 * K16)
+    act(A("nbI"), A("If"), scale=4096.0)
+    act(A("TH", 256, 384), A("If"), scale=A("pf", 5, 6))
+    act(A("Wo"), A("BOf"), scale=K16)
+    G8 = A("BOf", 0, 128, 16)
+    act(A("Wc", 0, 8), G8, scale=K16)
+    act(A("Wc", 8, 16), G8, scale=K16)
+    act(A("Wc", 16, 24), G8, scale=-2 * K16)
+    wmade = {}
+
+    def wts(a, b):
+        if (a, b) not in wmade:
+            j = 24 * len(wmade)
+            if (-a, -b) in wmade:
+                act(A("W", j, j + 24), wmade[(-a, -b)], scale=-1.0)
+            else:
+                for i, sc in enumerate((a, b, (a + b) * K16 / 2)):
+                    act(A("W", j + 8 * i, j + 8 * i + 8), G8, scale=float(sc))
+            wmade[(a, b)] = A("W", j, j + 24)
+        return wmade[(a, b)]
+    ms(A("crow", p=32), -240 * K16)
+    ms(A("crow", 16, 272, 17, p=32), -MID)
+    for h in range(2):
+        act(A("crow", 136 * h, 136 * h + 136, p=1), A("ioE", p=1), bias=-MID, scale=4096.0)
+    ts(A("I17"), A("ioF"), pc, None, ALU.is_equal)
+    ms(A("I17", 16, 136, 17), 0.0)
+    ms(A("crow", 16, 136, 17, p=1), -120 * K16)
+    ms(A("crow", 152, 272, 17, p=1), float(2 ** 25))
+    act(A("Q17"), A("I17"), scale=242 * K16)
+    ts(A("B17"), A("ioD"), gc, K16, ALU.is_equal, ALU.mult)
+    ms(A("B17", 16, 136, 17), 0.0)
+    ms(A("pw", 0, 16), 0.5)
+    ms(A("pw", 16, 32), 0.0)
+    scan(A("pw", 32, 48), A("pw", 0, 16), A("pw", 16, 32), K16, ALU.mult, ALU.add)
+    tt(A("pw", 0, 16), A("pw", 32, 48), A("RM", 0, 16), ALU.mult)
+    total(A("pf", 6, 7), A("pw", 0, 16))
+    ts(A("pf", 7, 8), A("pf", 6, 7), -8192.0, 4096.0, ALU.mult, ALU.add)
+    act(A("Wd"), A("BOf"), scale=A("pf", 6, 7))
+    ts(A("DM"), A("DM"), kc, None, ALU.add)
+    ts(A("CL"), A("DM"), float(R - V), None, ALU.add)
+    ts(A("DM"), A("DM"), C23, None, ALU.add)
+    ts(A("ExY", p=16), A("ioA", 0, 128, p=16), A("pf", 0, 1, p=16), None, ALU.is_equal)
+    ts(A("ExX", p=16), A("ioA", 0, 128, p=16), A("pf", 4, 5, p=16), None, ALU.is_equal)
+    cp(A("thf"), A("thi"))
+    ts(A("ngs", 0, 1), A("thf", 0, 1), -1.0, None, ALU.mult)
+    for c in (1, 0):
+        u0 = 32 * c
+        cp(A("LU", u0, u0 + 6), A("reci", 6 * c, 6 * c + 6))
+        ts(A("LU", u0 + 6, u0 + 12), A("reci", 6 * c, 6 * c + 6), 0.5, -0.25, ALU.mult, ALU.add)
+    cp(A("Pf", 0, V), A("Pi"))
+    X = A("XZ", 0, R)
+    Ib = A("I2", 0, 128)
+
+    def lanes(n, c, w=H, o=0, k=None):
+        return A(n, c * w + o, c * w + (w if k is None else o + k))
+
+    def red(out, c0, c1, step, data, c, wt, last=False):
+        mm([(A(out, c0 + k, c1, step, p=H), A(data, c * 1536 + k, (c + 1) * 1536, 16), wt, False, last and k == 15) for k in range(16)])
+
+    def piece(n, c, q):
+        return A(n, c * 1536 + 512 * q, c * 1536 + 512 * q + 512)
+
+    def prof(j, c, q):
+        return (ag if GE[9 * c + 3 * j + q] == "a" else vg)(piece("W" + "ABC"[j], c, q), X, lanes("ABC"[j] + "u", c, H, 32 * q, 32))
+
+    def dist(c, q, o, route, pairs, after):
+        Eq = P("E", 32 * q, 32 * q + 32, 0, 512)
+        rep = P("zpT", 32 * q, 32 * q + 32, 256 * c + o, 256 * c + o + 128)
+        if route == "m":
+            b = tile("r")
+            soft.append((after, mm([(A(b), rep, Eq, True, True)])))
+            for w, m in pairs:
+                tt(piece(m, c, q), A(b), piece(w, c, q), ALU.min)
+        else:
+            for w, m in pairs:
+                b = tile("r")
+                mm([(A(b), rep, Eq, True, False), (A(b), A("nIb"), piece(w, c, q), False, True)])
+                act(piece(m, c, q), A(b), AF.Abs)
+
+    for t in range(RO):
+        PW = A("Pi") if t == 0 else A("Pf", 0, V)
+        lu = lambda c, j, n=1: A("LU", t * 64 + 32 * c + 6 * j, t * 64 + 32 * c + 6 * (j + n))
+        zc = lambda c: A("ZL", t * L + H * c, t * L + H * c + H)
+        xb = lambda c: lanes("xy", c, 2 * H, 0, H)
+        yb = lambda c: lanes("xy", c, 2 * H, H, H)
+
+        def column(j, c, off):
+            n = "ABC"[j]
+            if FA[j] == "1":
+                ag(lanes(n + "f", c), A("Pf", 0, V), off)
+            else:
+                cp(lanes(n + "f", c), lanes(n + "u", c))
+
+        def head(c):
+            cur[0] = c
+            act(A("XZ", R + H * c, R + H * c + H), zc(c))
+            ag(lanes("rm", c), A("RM"), lu(c, 0))
+            b = tile("m")
+            mm([(A(b, 0, 128, p=H), zc(c), Ib, True, True)])
+            act(A("zpT", 256 * c, 256 * c + 128, p=H), A(b, 0, 128, p=H))
+            vg(lanes("Au", c), PW, lu(c, 1))
+            vg(lanes("M", c), PW, lu(c, 1), lanes("rm", c), ALU.mult)
+            b = tile("m")
+            mm([(A(b, 0, H), A("BOf"), lanes("M", c), True, False), (A(b, 0, H), Ib, A("ND", 0, H), False, True)])
+            scan(lanes("ys", c), A("RSn", 0, H), A(b, 0, H), 0.0, ALU.add, ALU.max)
+            ysl = A("ys", H * c + 15, H * c + H, 16)
+            ts(lu(c, 2), ysl, 0.5, -0.25, ALU.mult, ALU.add)
+            cp(lu(c, 3), ysl)
+            vg(lanes("Bu", c), PW, lu(c, 2))
+            ag(lanes("p", c), X, lu(c, 3))
+            b = tile("m")
+            mm([(A(b, 0, 128, p=H), lanes("p", c), Ib, True, True), (A(b, 128, 128 + H), A("BOf"), lanes("M", c), True, True)])
+            act(A("zpT", 256 * c + 128, 256 * c + 256, p=H), A(b, 0, 128, p=H))
+            act(yb(c), A(b, 128, 128 + H))
+            ag(xb(c), A("xtab"), lu(c, 0), -float(t))
+            act(lanes("rmf", c), lanes("rm", c))
+            act(lanes("nrm", c), lanes("rm", c), bias=1.0, scale=-1.0)
+            column(0, c, lu(c, 1))
+            column(1, c, lu(c, 2))
+            tt(lanes("eqab", c), lanes("Af", c), lanes("Bf", c), ALU.is_equal)
+            act(lanes("gxy", c, 2 * H), lanes("xy", c, 2 * H), bias=C23, scale=0.4999)
+            ts(A("gf", 16 * c, 16 * c + 12), lu(c, 1, 2), C23, None, ALU.add)
+
+        def stage_ab(c):
+            cur[0] = c
+            rz, rp = RAB[c]
+            KA = tile("k")
+            for q in range(3):
+                first = prof(0, c, q)
+                prof(1, c, q)
+                dist(c, q, 0, rz, (("WA", "MZA"), ("WB", "MZB")), first)
+                dist(c, q, 128, rp, (("WA", "MPA"), ("WB", "MPB")), first)
+            mm([(A(KA, 0, 384, p=H), A("ones", 0, H), A("TH"), True, False),
+                (A(KA, 0, 128, p=H), lanes("rm", c), A("penI"), False, False),
+                (A(KA, 0, 128, p=H), lanes("eqab", c), A("penI"), False, False),
+                (A(KA, 256, 384, p=H), lanes("Bf", c), A("If"), False, False)])
+            wa = (-1 if rz == "m" else 0, 1 if rp == "m" else 0)
+            za = 2 if rz == "m" else -1
+            pa = -2 if rp == "m" else 1
+            if wa != (0, 0):
+                red(KA, 0, 384, 16, "WA", c, wts(*wa))
+                red(KA, 0, 384, 16, "WB", c, wts(-wa[0], -wa[1]))
+            red(KA, 0, 384, 16, "MZA", c, wts(za, 0))
+            red(KA, 0, 384, 16, "MZB", c, wts(-za, 0))
+            red(KA, 0, 384, 16, "MPA", c, wts(0, pa))
+            red(KA, 0, 384, 16, "MPB", c, wts(0, -pa), True)
+            G0 = 256 * c
+            w = A("w", 128 * c, 128 * c + 128, p=H)
+            if WA_:
+                ga, gm = A("ga", 128 * c, 128 * c + 128, p=H), A("gm", 128 * c, 128 * c + 128, p=H)
+                act(ga, A(KA, 0, 128, p=H))
+                tt(gm, A(KA, 128, 256, p=H), ga, ALU.min)
+                act(w, gm, AF.Relu, bias=float(2 ** 25), scale=float(2 ** 25))
+            else:
+                act(A("G", G0, G0 + 256, p=H), A(KA, 0, 256, p=H), AF.Relu, bias=float(2 ** 25), scale=float(2 ** 25))
+                tt(w, A("G", G0, G0 + 128, p=H), A("G", G0 + 128, G0 + 256, p=H), ALU.min)
+            tt(A("key", 128 * c, 128 * c + 128, p=H), A(KA, 256, 384, p=H), w, ALU.min)
+
+        def mid(c):
+            cur[0] = c
+            s = lambda n, w=128, o=0, k=None, st=1: A(n, w * c + o, w * c + (w if k is None else o + k), st, p=H)
+            act(s("wit"), s("w"), AF.Sign)
+            scan(s("ks"), A("RSn", 0, 128, p=H), s("key"), 0.0, ALU.add, ALU.max)
+            scan(s("cs"), A("R01", p=H), s("wit"), 0.0, ALU.mult, ALU.add)
+            act(s("nbL", 8), s("cs", 128, 15, None, 16), AF.Sign, bias=-2.5)
+            kl = s("ks", 128, 15, None, 16)
+            ts(s("kf", 8), kl, RND, -RND, ALU.add, ALU.add)
+            b = tile("m")
+            mm([(A(b, 0, H, p=8), kl, A("If", 0, H, p=H), True, False)])
+            mm([(A(b, 0, H, p=8), s("kf", 8), A("nIf", 0, H, p=H), False, False),
+                (A(b, 0, H, p=8), s("nbL", 8), A("nbI", 0, H, p=H), False, True)])
+            act(A("vT", H * c, H * c + H, p=8), A(b, 0, H, p=8), bias=MID - 4096.0)
+            b = tile("m")
+            mm([(A(b, 0, H), A("ExY", p=8), A("vT", H * c, H * c + H, p=8), True, False), (A(b, 0, H), Ib, A("ND", 0, H), False, True)])
+            scan(lanes("vs", c), A("RSn", 0, H), A(b, 0, H), 0.0, ALU.add, ALU.max)
+            vl = A("vs", H * c + 15, H * c + H, 16)
+            ts(lanes("gC", c, 8, 0, 6), vl, 0.5, -0.25, ALU.mult, ALU.add)
+            vg(lanes("Cu", c), PW, lanes("gC", c, 8, 0, 6))
+            column(2, c, lanes("gC", c, 8, 0, 6))
+            tt(lanes("eqc", c, 2 * H, 0, H), lanes("Cf", c), yb(c), ALU.is_equal)
+            tt(lanes("eqc", c, 2 * H, H, H), lanes("Cf", c), xb(c), ALU.is_equal)
+            nb4 = lanes("nb4", c, 8, 0, 6)
+            act(nb4, vl, AF.Relu, scale=-1.0)
+            for r in range(2):
+                tt(lanes("s", c, 16, 6 * r, 6), lanes("gf", c, 16, 6 * r, 6), nb4, ALU.add)
+            tt(lanes("nbl", c, 8, 0, 6), nb4, A("CL", 12 * c, 12 * c + 6), ALU.min)
+
+        def dedup(c):
+            cur[0] = 0
+            b = tile("m")
+            lst = [(A(b, 0, 2 * H), Ib, A("ND"), True, False)]
+            for r in range(2):
+                e0 = (2 * c + r) * 6
+                ee = lambda j, a, z: (T.EE[:, e0 + j, a:z], "EE", (e0 + j) * 112 + a, (e0 + j) * 112 + z, z - a)
+                for j in range(6):
+                    n = H - 16 * j
+                    ts(ee(j, 0, n), lanes("gxy", c, 2 * H, r * H + 16 * j, n), lanes("s", c, 16, 6 * r + j, 1), None, ALU.is_equal)
+                    if n > 16:
+                        lst.append((A(b, r * H + 16 * j + 16, r * H + H), A("Wo"), ee(j, 16, n), False, False))
+                lst.append((A(b, r * H, r * H + H), A("Wd"), (T.EE[:, e0:e0 + 6, 0:16], "EE", e0 * 112, (e0 + 6) * 112, H), False, r == 1))
+            mm(lst)
+            scan(lanes("ds", c, 2 * H), A("RSn"), A(b, 0, 2 * H), 0.0, ALU.add, ALU.max)
+            q = lambda n: lanes(n, c, 16, 0, 12)
+            act(q("t1"), A("ds", 2 * H * c + 15, 2 * H * (c + 1), 16), AF.Relu, bias=A("pf", 7, 8), scale=4096.0)
+            tt(q("t2"), q("t1"), q("s"), ALU.add)
+            tt(q("t3"), q("t2"), A("DM", 12 * c, 12 * c + 12), ALU.min)
+            ts(q("off"), q("t3"), -C23, None, ALU.add)
+
+        def count():
+            b = tile("m")
+            mm([(A(b, 0, 16), A("ones", p=H), A("nbL", p=H), True, True)])
+            total(A("cn", 0, 1), A(b, 0, 16))
+            ts(A("ci", 0, 1), A("cn", 0, 1), 0.5, 4.0 * L, ALU.mult, ALU.add)
+            ts(A("ci", 1, 2), A("ci", 0, 1), 15, None, ALU.bitwise_and)
+            ts(A("ngs", t + 1, t + 2), A("ci", 1, 2), A("thf", t + 1, t + 2), -1.0, ALU.add, ALU.mult)
+
+        def stage_c(c):
+            cur[0] = c
+            rz, rp = RC[c]
+            KC = tile("k")
+            for q in range(3):
+                first = prof(2, c, q)
+                dist(c, q, 0, rz, (("WC", "MZC"),), first)
+                dist(c, q, 128, rp, (("WC", "DPC"),), first)
+            G1 = A("If", 0, 128, 16)
+            lst = [(A(KC, 0, 272, p=H), A("ones", 0, H, p=2), A("crow", p=2), True, False),
+                   (A(KC, 16, 136, 17, p=H), A("brI", 0, H, p=H), A("nbL", 8 * c, 8 * c + 8, p=H), False, False),
+                   (A(KC, 16, 136, 17, p=H), yb(c), G1, False, False)]
+            for o, route, own in ((0, rz, zc(c)), (136, rp, lanes("p", c))):
+                if route == "m":
+                    lst.append((A(KC, o, o + 136, p=H), own, A("B17"), False, False))
+            mm(lst)
+            for o in (0, 136):
+                mm([(A(KC, o, o + 136, p=H), lanes("Cf", c), A("I17"), False, False)])
+            if "m" in (rz, rp):
+                red(KC, 0 if rz == "m" else 136, 272 if rp == "m" else 136, 17, "WC", c, A("Wc", 0, 16 if rz == rp else 8))
+            red(KC, 0, 136, 17, "MZC", c, A("Wc", 16, 24) if rz == "m" else A("Wc", 0, 8))
+            if rp == "m":
+                red(KC, 136, 272, 17, "DPC", c, A("Wc", 16, 24))
+            mm([(A(KC, 0, 136, p=H), lanes("eqc", c, 2 * H, 0, H), A("Q17"), False, False),
+                (A(KC, 136, 272, p=H), lanes("eqc", c, 2 * H, H, H), A("Q17"), False, rp == "m")])
+            if rp == "a":
+                red(KC, 136, 272, 17, "DPC", c, A("Wc", 0, 8), True)
+            scan(A("ks2", 272 * c, 272 * c + 272, p=H), A("RS17", p=H), A(KC, 0, 272, p=H), 0.0, ALU.add, ALU.min)
+
+        def tail(c):
+            cur[0] = c
+            kl = A("ks2", 272 * c + 16, 272 * c + 272, 17, p=H)
+            yf = A("yf", 16 * c, 16 * c + 16, p=H)
+            k2 = len(ops)
+            ts(yf, kl, RND, -RND, ALU.add, ALU.add)
+            b = tile("m")
+            mm([(A(b, 0, H, p=16), kl, A("If", 0, H, p=H), True, False)])
+            mm([(A(b, 0, H, p=16), yf, A("nIf", 0, H, p=H), False, True)])
+            vT = A("vT2", H * c, H * c + H, p=16)
+            act(vT, A(b, 0, H, p=16), bias=MID)
+            b = tile("m")
+            soft.append((k2, mm([(A(b, 0, H), A("nIf"), yb(c), True, False)])))
+            mm([(A(b, 0, H), A("ExY", p=16), vT, False, True)])
+            tt(lanes("Ym", c), A(b, 0, H), lanes("rmf", c), ALU.mult)
+            vscat(A("Pf"), lanes("off", c, 16, 0, 6), lanes("Ym", c), lanes("Af", c))
+            b = tile("m")
+            mm([(A(b, 0, H), A("ExX", p=16), vT, True, True),
+                (A(b, H, 2 * H), Ib, A("ND", 0, H), True, False), (A(b, H, 2 * H), A("ExY", p=16), vT, False, True)])
+            tt(lanes("Xm", c), A(b, 0, H), lanes("rmf", c), ALU.mult)
+            scan(lanes("xs", c), A("RSn", 0, H), A(b, H, 2 * H), 0.0, ALU.add, ALU.max)
+            xl = A("xs", H * c + 15, H * c + H, 16)
+            u0 = t * 64 + 32 * c
+            if t + 1 < RO:
+                ts(A("SU", u0, u0 + 6), xl, float(t + 1), None, ALU.add)
+                ts(A("SU", u0 + 6, u0 + 12), xl, 0.5, -0.25, ALU.mult, ALU.add)
+                send(rank + 1, A("SU", u0, u0 + 12), A("LU", u0 + 64, u0 + 76), "ax%d%d" % (t + 1, c))
+            else:
+                cp(A("XF", 8 * c, 8 * c + 6), xl)
+                send(rank - t, A("XF", 8 * c, 8 * c + 6), A("XL", 8 * c, 8 * c + 6), "ax%d%d" % (t + 1, c))
+            tt(lanes("wof", c, 8, 0, 6), xl, lanes("nbl", c, 8, 0, 6), ALU.max)
+            cp(lanes("wou", c, 8, 0, 6), lanes("wof", c, 8, 0, 6))
+            if ZA:
+                ag(lanes("zw", c), A("XZ"), lanes("wou", c, 8, 0, 6))
+                b = tile("m")
+                mm([(A(b, 0, H), Ib, zc(c), True, False), (A(b, 0, H), Ib, lanes("zw", c), False, True)])
+                act(lanes("zr", c), A(b, 0, H), bias=191.75, scale=0.5)
+            else:
+                vg(lanes("zs", c), A("XZ"), lanes("wou", c, 8, 0, 6), zc(c), ALU.add)
+                act(lanes("zr", c), lanes("zs", c), bias=191.75, scale=0.5)
+            z0 = t * L + H * c
+            act(A("ZS", z0, z0 + H), lanes("zr", c), bias=-192.0)
+            send(rank + 1 if t + 1 < RO else rank - t, A("ZS", z0, z0 + H), A("ZL", z0 + L, z0 + L + H), "az%d%d" % (t + 1, c))
+
+        occ.clear()
+        act(A("TH", 0, 256), A("I2"), scale=A("ngs", t, t + 1))
+        head(1)
+        head(0)
+        stage_ab(1)
+        mid(1)
+        stage_ab(0)
+        dedup(1)
+        mid(0)
+        if t + 1 < RO:
+            count()
+        dedup(0)
+        stage_c(1)
+        tail(1)
+        stage_c(0)
+        tail(0)
+        for c in (1, 0):
+            vg(lanes("B1", c), A("Pf", 0, V), lu(c, 2), lanes("nrm", c), ALU.mult)
+        for c in (1, 0):
+            vscat(A("Pf"), lanes("off", c, 16, 6, 6), lanes("Xm", c), lanes("B1", c))
+
+    dma("s", T.ypar[:], T.Pf[:, 0:V], [A("Pf", 0, V)], [], 4000.0)
+    for c in (1, 0):
+        z0 = RO * L + H * c
+        dma("s", T.yrec[:, 6 * c:6 * c + 6], T.XL[:, 8 * c:8 * c + 6], [A("XL", 8 * c, 8 * c + 6)], [], 2000.0)
+        dma("a", T.yz[:, H * c:H * c + H], T.ZL[:, z0:z0 + H], [A("ZL", z0, z0 + H)], [], 2000.0)
+
+    n = len(ops)
+    succ = [[] for _ in range(n)]
+    for i, o in enumerate(ops):
+        for d in o[4]:
+            succ[d].append(i)
+    prio = [0.0] * n
+    for i in range(n - 1, -1, -1):
+        prio[i] = ops[i][1] + ops[i][2] + max([prio[j] + (HOP if ops[j][4][i] else 0.0) for j in succ[i]] + [0.0])
+    extra = {}
+    for w in PRI.split():
+        k = max(w.rfind("+"), w.rfind("-"))
+        extra[w[:k]] = 1000.0 * int(w[k:])
+    prio = [prio[i] + BIAS * ops[i][9] + extra.get(ops[i][8][:-2][:2] + ops[i][8][-2], 0.0) for i in range(n)]
+    left = [len(o[4]) for o in ops]
+    softs = [[] for _ in range(n)]
+    for a, b in soft:
+        softs[a].append(b)
+        left[b] += 1
+    opens = {u[0]: nm for nm, u in users.items()}
+    uses = [[] for _ in range(n)]
+    for nm, u in users.items():
+        for i in u:
+            uses[i].append(nm)
+    todo = {nm: len(u) for nm, u in users.items()}
+    bank_of, holder, bfree, held = {}, [None] * 8, [0.0] * 8, {"r": 0, "k": 0, "m": 0}
+    idle = list(range(8))
+    tfin = {nm: 0.0 for nm in users}
+    ready_t = [0.0] * n
+    cand = [i for i in range(n) if left[i] == 0]
+    free = {e: 0.0 for e in "vapgsx"}
+    order = []
+    tend = 0.0
+
+    def start(i):
+        s0 = max(ready_t[i], free[ops[i][0]])
+        if i in opens:
+            if not idle or held[opens[i][1]] >= CAP[opens[i][1]]:
+                return 1e18
+            s0 = max(s0, min(bfree[b] for b in idle))
+        return s0
+    while cand:
+        best = min(cand, key=lambda i: (round(start(i) / GRAIN), -prio[i]))
+        e = ops[best][0]
+        st = start(best)
+        assert st < 1e17
+        cand.remove(best)
+        order.append((best, st))
+        if best in opens:
+            nm = opens[best]
+            b = min(idle, key=lambda x: bfree[x])
+            idle.remove(b)
+            held[nm[1]] += 1
+            bank_of[nm] = b
+            if holder[b] is not None:
+                for u in users[holder[b]]:
+                    if ops[u][0] != "p":
+                        ops[best][4][u] = True
+                        succ[u].append(best)
+            holder[b] = nm
+        if e != "x":
+            free[e] = st + ops[best][1]
+        fin = st + ops[best][1] + ops[best][2]
+        tend = max(tend, fin)
+        for nm in uses[best]:
+            todo[nm] -= 1
+            tfin[nm] = max(tfin[nm], fin + HOP)
+            if todo[nm] == 0:
+                idle.append(bank_of[nm])
+                bfree[bank_of[nm]] = tfin[nm]
+                held[nm[1]] -= 1
+        for j in softs[best] + succ[best]:
+            now = j in softs[best] or (ops[j][0] == e and not ops[j][4][best])
+            ready_t[j] = max(ready_t[j], st if now else fin + HOP)
+            left[j] -= 1
+            if left[j] == 0:
+                cand.append(j)
+    for a in lazy:
+        a[0] = T[BANKS[bank_of[a[1]]]][0:a[6], a[2]:a[3]:a[5]] if a[5] > 1 else T[BANKS[bank_of[a[1]]]][0:a[6], a[2]:a[3]]
+
+    marked = [any(ops[j][4][i] for j in succ[i]) for i in range(n)]
+    csem = {"v": T.sem.cv, "a": T.sem.ca, "p": T.sem.cp, "g": T.sem.cg}
+    tick = {e: 0 for e in csem}
+    stamp = [0] * n
+    seen = {e: {} for e in Q}
+    for i, st in order:
+        e, cost, lat, fn, deps, kind, sem, cnt = ops[i][:8]
+        if kind == "x":
+            continue
+        need = {}
+        for d, w in deps.items():
+            if w:
+                key = ops[d][0] if ops[d][5] == "c" else d
+                need[key] = max(need.get(key, 0), stamp[d] if ops[d][5] == "c" else ops[d][7])
+        for key, val in need.items():
+            if seen[e].get(key, 0) < val:
+                Q[e].wait_ge(csem[key] if key in csem else ops[key][6], val)
+                seen[e][key] = val
+        ins = fn(Q[e])
+        if kind == "c" and marked[i]:
+            tick[e] += 1
+            stamp[i] = tick[e]
+            ins.then_inc(csem[e], 1)
+    for e in csem:
+        g.sync.wait_ge(csem[e], tick[e])
+    for o in ops:
+        if o[5] == "d":
+            g.sync.wait_ge(o[6], o[7])
+    g.wait_ge(T.sem.sent, sent[0])
+    return (tend, order, ops)

@@ -9,9 +9,10 @@ MID = 1280.0
 RND = 1.5 * 2 ** 35
 RAB = [("m", "m"), ("m", "m")]
 RC = [("m", "a"), ("a", "m")]
-GE = "aaaaaaavaaavaaavaa"
-FA = "001"
-ZA, WA_ = 1, 1
+GE = "aaaaaaavavaaaaaava"
+FA = "101"
+SPLIT = ""
+ZA, WA_ = 0, 1
 
 F, B, I, U = "float32", "bfloat16", "int32", "uint16"
 SB = {
@@ -44,14 +45,14 @@ ARR = ["a%s%d%d" % (k, t, c) for k in "xz" for t in range(1, RO + 1) for c in ra
 DMAS = ["d%d" % i for i in range(12)]
 SEMAPHORES = ["cv", "ca", "cp", "cg", "sent"] + ARR + DMAS
 
-CY, PC, GA, SC, HOP = 0.83 * 1.2, 0.42 * 1.2, 1.56, 3.8, 80.0
-GRAIN, BIAS = 20.0, 3000.0
+CY, PC, GA, SC, HOP = 0.83 * 1.2, 0.42 * 1.2, 1.56, 3.8, 140.0
+GRAIN, BIAS = 20.0, 5000.0
 CAP = {"r": 5, "k": 2, "m": 8}
-PRI = ("t30-3 ga0+1 w0-3 G0+1 WA0+1 Au0-6 WB1+6 ds1+6 zr1-6 Xm1-6 t10+9 yf0+9 TH1-1 SU0+6 SU1-6 zw1+6 gC1+6 LU0-3 EE0-1 wo1+3 ke0+3 "
-       "Cu1+6 ZS0+3 Bf1+3 yf1+9 nb1-1 rm1+9 MP1-1 DP1-3 vs1+1 Pf1+6 Ym1-1 zr0-3 wi1-1 Au1-3 nr1-3 ds0+6 of0-6 vs0-6 zs1-1 gf0+3 WA1-1 "
-       "Ym0-1 nb0-6 xy0+9 wi0-6 MZ1-6 ks0-6 gm1-1 eq0+6 vT1+3 Bu1-3 kf0+3 xy1+9 rm0-1 zp0+1 xs0+6 XZ1+6 Cf1+1 EE1+1 ga1-6 gf1-6 Bf0+3 "
-       "ke1+6 ys1+6 cs1+9 t20-3 gC0+3 zw0+6 M1+6 cs0+3 PZ1-1 Xm0-6 ks1+9 PB0-1 eq1+9 Po1-3 t31+3 Py0+1 gx0+9 w1-3 wo0-1 DP0+6 Pz0+9 "
-       "XZ0-3 Pp0+6 of1+9 B11+3 G1+6 Pk0-1 Pn0-1")
+PRI = ("t30-1 ga0+3 w0+1 G0+1 Au0-6 WB1+6 yf0+9 SU0+3 SU1-6 zw1+6 LU0-3 EE0-1 wo1-6 ke0+3 Cu1+6 ZS0+1 Bf1+3 yf1-3 nb1-1 DP1-3 vs1+6 "
+       "Pf1+9 Ym1-1 zr0+6 wi1-1 Au1+6 nr1-3 ds0+6 vs0+1 WA1-1 nb0-6 xy0+1 wi0-6 MZ1-6 ks0-1 eq0+3 xy1+9 rm0-1 zp0+1 xs0+9 Cf1-3 EE1-1 "
+       "ga1-3 gf1-6 Bf0+3 ys1+1 t20+9 zw0+1 PZ1+9 ks1+6 Po1+1 Py0+6 wo0-1 Pz0+9 Pp0+6 p0-3 PB1+1 ys0+6 PI1+1 s0+3 w1+6 kf0+9 gx1-1 "
+       "PC1+9 Pn1+9 Bu0-3 vT0+6 MP1+1 t21-6 PD0+6 Xm0-6 Af1+9 Po0+1 Pe0+1 S1+9 PZ0-1 Bu1+9 t11+1 Py1+3 PD1+3 PM0+6 t31-1 Pz1+1 Pf0+9 "
+       "PE0+9 XZ0-1 S0+6 cs0+3 TH1+1 XZ1-6 WC0-3 zs0+1 G1+9 Af0-3 zs1-3 B10+3 of1+1 eq1+6 Xm1+3 s1+3 ZS1+3 Pk0+1")
 
 
 def rank_program(g, core, T, topo):
@@ -65,10 +66,10 @@ def rank_program(g, core, T, topo):
     acc = {}
     lazy, soft, users, cur, nt, nd, sent = [], [], {}, [0], [0], [0], [0]
 
-    def A(n, c0=0, c1=None, st=1, p=128):
+    def A(n, c0=0, c1=None, st=1, p=128, p0=0):
         if n[0] == "#":
             c1 = 512 if c1 is None else c1
-            a = [None, n, c0, c1, len(range(c0, c1, st)), st, p]
+            a = [None, n, c0, c1, len(range(c0, c1, st)), st, p, p0]
             lazy.append(a)
             return a
         c1 = SB[n][0] if c1 is None else c1
@@ -150,7 +151,7 @@ def rank_program(g, core, T, topo):
 
     def vscat(win, off, a, b):
         add("v", 50 + a[4] * SC * CY, [off, a, b], [win],
-            lambda q: q.tensor_tensor(win[0].indirect(off[0]), a[0], b[0], ALU.add), tag="s")
+            lambda q: q.tensor_tensor(win[0].indirect(off[0]), a[0], b[0], ALU.max), tag="s")
 
     def act(o, i, f=AF.Identity, bias=0.0, scale=1.0):
         rd = [i] + [s for s in (bias, scale) if isinstance(s, tuple)]
@@ -196,14 +197,16 @@ def rank_program(g, core, T, topo):
         ne = len(topo.engines(core, dst))
         sent[0] += ne
         me = add("g", 900.0, [src], [], lambda q: q.remote_dma(land[0], src[0], T.sem[name], T.sem.sent, pid, rid, mask), kind="r")
-        o = add("x", 0.0, [], [land], None, kind="x", lat=2500.0, sem=T.sem[name], cnt=ne)
+        o = add("x", 0.0, [], [land], None, kind="x", lat=3200.0, sem=T.sem[name], cnt=ne)
         ops[o][4][me] = False
 
-    dma("s", T.reci[:], T.rec[:], [], [A("reci")], 2000.0)
-    dma("s", T.Pi[:], T.par[:], [], [A("Pi")], 4000.0)
-    dma("a", T.XZ[:, 0:R], T.prof[:], [], [A("XZ", 0, R)], 4000.0)
-    dma("s", T.ZL[:, 0:L], T.zf[:], [], [A("ZL", 0, L)], 2500.0)
-    dma("s", T.thi[:], T.th[:], [], [A("thi")], 2500.0)
+    dma("a", T.reci[:], T.rec[:], [], [A("reci")], 2000.0)
+    first = len(ops)
+    dma("s", T.Pi[:], T.par[:], [], [A("Pi")], 3500.0)
+    dma("s", T.XZ[:, 0:R], T.prof[:], [], [A("XZ", 0, R)], 5000.0)
+    soft.append((first, first + 1))
+    dma("a", T.ZL[:, 0:L], T.zf[:], [], [A("ZL", 0, L)], 2500.0)
+    dma("a", T.thi[:], T.th[:], [], [A("thi")], 2500.0)
 
     iota(A("pi", 0, 1), [[0, 1]], 0, 1)
     iota(A("ioC"), [[0, 6], [1, 16]], 0, 0)
@@ -301,6 +304,11 @@ def rank_program(g, core, T, topo):
         return A(n, c * w + o, c * w + (w if k is None else o + k))
 
     def red(out, c0, c1, step, data, c, wt, last=False):
+        if data + str(c) in SPLIT:
+            mm([(A(out, c0 + k, c1, step, p=64), A(data, c * 1536 + k, c * 1536 + 1024, 16), wt, False, False) for k in range(16)])
+            mm([(A(out, c0 + k, c1, step, p=H, p0=64), A(data, c * 1536 + 1024 + k, (c + 1) * 1536, 16), wt, False, last and k == 15)
+                for k in range(16)])
+            return
         mm([(A(out, c0 + k, c1, step, p=H), A(data, c * 1536 + k, (c + 1) * 1536, 16), wt, False, last and k == 15) for k in range(16)])
 
     def piece(n, c, q):
@@ -359,9 +367,8 @@ def rank_program(g, core, T, topo):
             act(A("zpT", 256 * c + 128, 256 * c + 256, p=H), A(b, 0, 128, p=H))
             act(yb(c), A(b, 128, 128 + H))
             ag(xb(c), A("xtab"), lu(c, 0), -float(t))
-            act(lanes("rmf", c), lanes("rm", c))
             act(lanes("nrm", c), lanes("rm", c), bias=1.0, scale=-1.0)
-            column(0, c, lu(c, 1))
+            vg(lanes("Af", c), PW, lu(c, 1), lanes("nrm", c), ALU.mult)
             column(1, c, lu(c, 2))
             tt(lanes("eqab", c), lanes("Af", c), lanes("Bf", c), ALU.is_equal)
             act(lanes("gxy", c, 2 * H), lanes("xy", c, 2 * H), bias=C23, scale=0.4999)
@@ -493,7 +500,6 @@ def rank_program(g, core, T, topo):
             cur[0] = c
             kl = A("ks2", 272 * c + 16, 272 * c + 272, 17, p=H)
             yf = A("yf", 16 * c, 16 * c + 16, p=H)
-            k2 = len(ops)
             ts(yf, kl, RND, -RND, ALU.add, ALU.add)
             b = tile("m")
             mm([(A(b, 0, H, p=16), kl, A("If", 0, H, p=H), True, False)])
@@ -501,14 +507,14 @@ def rank_program(g, core, T, topo):
             vT = A("vT2", H * c, H * c + H, p=16)
             act(vT, A(b, 0, H, p=16), bias=MID)
             b = tile("m")
-            soft.append((k2, mm([(A(b, 0, H), A("nIf"), yb(c), True, False)])))
-            mm([(A(b, 0, H), A("ExY", p=16), vT, False, True)])
-            tt(lanes("Ym", c), A(b, 0, H), lanes("rmf", c), ALU.mult)
+            mm([(A(b, 0, H), A("nbI"), lanes("rm", c), True, False), (A(b, 0, H), A("ExY", p=16), vT, False, True)])
+            act(lanes("Ym", c), A(b, 0, H), bias=-4096.0)
             vscat(A("Pf"), lanes("off", c, 16, 0, 6), lanes("Ym", c), lanes("Af", c))
             b = tile("m")
-            mm([(A(b, 0, H), A("ExX", p=16), vT, True, True),
-                (A(b, H, 2 * H), Ib, A("ND", 0, H), True, False), (A(b, H, 2 * H), A("ExY", p=16), vT, False, True)])
-            tt(lanes("Xm", c), A(b, 0, H), lanes("rmf", c), ALU.mult)
+            mm([(A(b, 0, H), A("nbI"), lanes("rm", c), True, False), (A(b, 0, H), A("ExX", p=16), vT, False, True)])
+            act(lanes("Xm", c), A(b, 0, H), bias=-4096.0)
+            b = tile("m")
+            mm([(A(b, H, 2 * H), Ib, A("ND", 0, H), True, False), (A(b, H, 2 * H), A("ExY", p=16), vT, False, True)])
             scan(lanes("xs", c), A("RSn", 0, H), A(b, H, 2 * H), 0.0, ALU.add, ALU.max)
             xl = A("xs", H * c + 15, H * c + H, 16)
             u0 = t * 64 + 32 * c
@@ -637,7 +643,7 @@ def rank_program(g, core, T, topo):
             if left[j] == 0:
                 cand.append(j)
     for a in lazy:
-        a[0] = T[BANKS[bank_of[a[1]]]][0:a[6], a[2]:a[3]:a[5]] if a[5] > 1 else T[BANKS[bank_of[a[1]]]][0:a[6], a[2]:a[3]]
+        a[0] = T[BANKS[bank_of[a[1]]]][a[7]:a[6], a[2]:a[3]:a[5]] if a[5] > 1 else T[BANKS[bank_of[a[1]]]][a[7]:a[6], a[2]:a[3]]
 
     marked = [any(ops[j][4][i] for j in succ[i]) for i in range(n)]
     csem = {"v": T.sem.cv, "a": T.sem.ca, "p": T.sem.cp, "g": T.sem.cg}

from concourse.mybir import AluOpType as ALU, AxisListType as AX, ActivationFunctionType as AF

V, R, L, RO = 1280, 2560, 192, 4
H = 96
BIG = float(2 ** 26)
K16 = 65536.0
C23 = 1.5 * 2 ** 23
MID = 1280.0
RND = 1.5 * 2 ** 35
RAB = [("m", "m"), ("m", "m")]
RC = [("m", "a"), ("a", "m")]
GE = "aaaaaaavavaaaaaava"
FA = "101"
SPLIT = ""
ZA, WA_ = 0, 1

F, B, I, U = "float32", "bfloat16", "int32", "uint16"
SB = {
    "XZ": (R + L, B), "Pi": (V, I), "Pf": (V + L, F), "thi": (4, I), "thf": (4, F), "reci": (12, I),
    "xtab": (R + 4, F), "RM": (2576, B),
    "pi": (4, I), "pf": (8, F), "ioA": (512, F), "ioB": (128, F), "ioC": (96, F), "ioD": (136, F), "ioE": (136, F),
    "ioF": (136, F), "E": (512, B), "BOf": (128, F), "If": (128, F), "nIf": (128, F), "I2": (256, B), "nIb": (128, B), "penI": (128, B),
    "brI": (128, B), "ones": (128, B), "ND": (192, B), "RSn": (192, F), "RS17": (272, F), "R01": (128, B), "I17": (136, F),
    "Q17": (136, B), "B17": (136, B), "crow": (272, B), "W": (24 * 16, B), "Wc": (24, B), "nbI": (128, B),
    "Wd": (128, B), "Wo": (128, B), "pw": (48, F), "DM": (24, F), "CL": (24, F), "ExY": (128, F), "ExX": (128, F), "TH": (384, B),
    "LU": (RO * 64, U), "SU": (RO * 64, U), "ZL": ((RO + 1) * L, B), "ZS": (RO * L, B), "XF": (16, F), "XL": (16, F),
    "Au": (L, U), "Bu": (L, U), "Cu": (L, U), "Af": (L, F), "Bf": (L, F), "Cf": (L, F), "M": (L, F), "rm": (L, B), "nrm": (L, F),
    "rmf": (L, F), "xy": (2 * L, F), "gxy": (2 * L, F), "ys": (L, F), "p": (L, B), "zpT": (512, B), "eqab": (L, B), "eqc": (2 * L, B),
    "WA": (16 * L, B), "WB": (16 * L, B), "WC": (16 * L, B), "MZA": (16 * L, B), "MZB": (16 * L, B), "MPA": (16 * L, B),
    "MPB": (16 * L, B), "MZC": (16 * L, B), "DPC": (16 * L, B),
    "G": (512, B), "w": (256, B), "key": (256, F), "wit": (256, B), "ks": (256, F), "cs": (256, B), "nbL": (16, B),
    "kf": (16, F), "vT": (L, F), "vs": (L, F), "gC": (16, U), "nb4": (16, F), "gf": (32, F), "s": (32, F),
    "nbl": (16, F), "ds": (2 * L, F), "t1": (32, F), "t2": (32, F), "t3": (32, F), "off": (32, U),
    "ks2": (544, F), "yf": (32, F), "vT2": (L, F), "Ym": (L, F), "Xm": (L, F), "B1": (L, F),
    "xs": (L, F), "wof": (16, F), "wou": (16, U), "zs": (L, F), "zr": (L, B), "zw": (L, B), "ga": (256, F), "gm": (256, F),
    "cn": (4, F), "ci": (4, I), "ngs": (4, F),
}
BANKS = ["bank%d" % i for i in range(8)]
SCRATCH = {n: ("sbuf", [128, w], d) for n, (w, d) in SB.items()}
SCRATCH["EE"] = ("sbuf", [128, 24, 112], B)
SB["EE"] = (24 * 112, B)
for _b in BANKS:
    SCRATCH[_b] = ("psum", [128, 512], F)
ARR = ["a%s%d%d" % (k, t, c) for k in "xz" for t in range(1, RO + 1) for c in range(2)]
DMAS = ["d%d" % i for i in range(12)]
SEMAPHORES = ["cv", "ca", "cp", "cg", "sent"] + ARR + DMAS

CY, PC, GA, SC, HOP = 0.83 * 1.2, 0.42 * 1.2, 1.56, 3.8, 140.0
GRAIN, BIAS = 20.0, 5000.0
CAP = {"r": 5, "k": 2, "m": 8}
PRI = ("t30-1 ga0+3 w0+1 G0+1 Au0-6 WB1+6 yf0+9 SU0+3 SU1-6 zw1+6 LU0-3 EE0-1 wo1-6 ke0+3 Cu1+6 ZS0+1 Bf1+3 yf1-3 nb1-1 DP1-3 vs1+6 "
       "Pf1+9 Ym1-1 zr0+6 wi1-1 Au1+6 nr1-3 ds0+6 vs0+1 WA1-1 nb0-6 xy0+1 wi0-6 MZ1-6 ks0-1 eq0+3 xy1+9 rm0-1 zp0+1 xs0+9 Cf1-3 EE1-1 "
       "ga1-3 gf1-6 Bf0+3 ys1+1 t20+9 zw0+1 PZ1+9 ks1+6 Po1+1 Py0+6 wo0-1 Pz0+9 Pp0+6 p0-3 PB1+1 ys0+6 PI1+1 s0+3 w1+6 kf0+9 gx1-1 "
       "PC1+9 Pn1+9 Bu0-3 vT0+6 MP1+1 t21-6 PD0+6 Xm0-6 Af1+9 Po0+1 Pe0+1 S1+9 PZ0-1 Bu1+9 t11+1 Py1+3 PD1+3 PM0+6 t31-1 Pz1+1 Pf0+9 "
       "PE0+9 XZ0-1 S0+6 cs0+3 TH1+1 XZ1-6 WC0-3 zs0+1 G1+9 Af0-3 zs1-3 B10+3 of1+1 eq1+6 Xm1+3 s1+3 ZS1+3 Pk0+1")


def rank_program(g, core, T, topo):
    rank = T.rank_of(core)
    if rank is None:
        return
    n_r = len(T.cores)
    Q = {"v": g.vector, "a": g.scalar, "p": g.tensor, "g": g, "s": g.sync}
    ops = []
    occ = {}
    acc = {}
    lazy, soft, users, cur, nt, nd, sent = [], [], {}, [0], [0], [0], [0]

    def A(n, c0=0, c1=None, st=1, p=128, p0=0):
        if n[0] == "#":
            c1 = 512 if c1 is None else c1
            a = [None, n, c0, c1, len(range(c0, c1, st)), st, p, p0]
            lazy.append(a)
            return a
        c1 = SB[n][0] if c1 is None else c1
        ap = T[n][0:p, c0:c1:st] if st > 1 else T[n][0:p, c0:c1]
        return (ap, n, c0, c1, len(range(c0, c1, st)))

    def P(n, p0, p1, c0, c1):
        return (T[n][p0:p1, c0:c1], n, c0, c1, c1 - c0)

    def tile(kind):
        nt[0] += 1
        return "#%s%d" % (kind, nt[0])

    def add(e, cost, rd, wr, fn, kind="c", lat=0.0, sem=None, cnt=0, tag=""):
        me = len(ops)
        deps = {}
        for a, isw in [(a, False) for a in rd] + [(a, True) for a in wr]:
            n, c0, c1 = a[1], a[2], a[3]
            ps = n[0] == "#"
            if ps:
                users.setdefault(n, [])
                if me not in users[n]:
                    users[n].append(me)
                c0, c1 = 0, 512
            keep = []
            for (o, d0, d1, w) in acc.get(n, []):
                hit = o != me and d0 < c1 and c0 < d1
                same = hit and ops[o][0] == e and ops[o][5] == "c" and kind == "c"
                if hit and (w or isw or (ps and not same)):
                    deps[o] = deps.get(o, False) or not (same and e == "p")
                if not (hit and (isw or ps) and c0 <= d0 and d1 <= c1 and (isw or not (w or same))):
                    keep.append((o, d0, d1, w))
            keep.append((me, c0, c1, isw))
            acc[n] = keep
        nm = ("P" + rd[0][1] if e == "p" else wr[0][1] if wr else "S") + str(cur[0])
        occ[nm] = occ.get(nm, 0) + 1
        ops.append([e, cost, lat, fn, deps, kind, sem, cnt, nm + "abcdefghijklmnopqrstuvwxyz"[min(occ[nm] - 1, 25)], cur[0], tag])
        return me

    def two(*xs):
        return all(x[1][0] != "#" and SB[x[1]][1] in (B, U) for x in xs)

    def vcost(n, f=1.0):
        return max(64.0, n * f) * CY + 20

    def ts(o, i, s1, s2, o0, o1=None):
        rd = [i] + [s for s in (s1, s2) if isinstance(s, tuple)]
        a1 = s1[0] if isinstance(s1, tuple) else s1
        a2 = s2[0] if isinstance(s2, tuple) else s2
        if o1 is None:
            fn = lambda q: q.tensor_scalar(o[0], i[0], a1, None, o0)
        else:
            fn = lambda q: q.tensor_scalar(o[0], i[0], a1, a2, o0, o1)
        add("v", vcost(o[4], 0.5 if two(o, i) else 1), rd, [o], fn)

    def cp(o, i):
        add("v", vcost(o[4], 0.5 if two(o, i) else 1), [i], [o], lambda q: q.tensor_copy(o[0], i[0]))

    def ms(o, val):
        add("v", vcost(o[4], 0.5 if two(o) else 1), [], [o], lambda q: q.memset(o[0], val))

    def tt(o, a, b, op):
        f = 1 if "#" in (a[1][0], b[1][0]) else 2
        add("v", vcost(o[4], f), [a, b], [o], lambda q: q.tensor_tensor(o[0], a[0], b[0], op))

    def scan(o, d0, d1, init, o0, o1):
        add("v", vcost(o[4], 0.5 if two(o, d0, d1) else 1), [d0, d1], [o],
            lambda q: q.tensor_tensor_scan(o[0], d0[0], d1[0], init, o0, o1))

    def total(o, i):
        add("v", 80.0, [i], [o], lambda q: q.tensor_reduce(o[0], i[0], AX.X, ALU.add))

    def vg(o, win, off, b=None, op=None):
        if b is None:
            fn = lambda q: q.tensor_copy(o[0], win[0].indirect(off[0]))
        else:
            fn = lambda q: q.tensor_tensor(o[0], win[0].indirect(off[0]), b[0], op)
        return add("v", 50 + o[4] * GA * CY, [win, off] + ([b] if b else []), [o], fn, tag="g")

    def vscat(win, off, a, b):
        add("v", 50 + a[4] * SC * CY, [off, a, b], [win],
            lambda q: q.tensor_tensor(win[0].indirect(off[0]), a[0], b[0], ALU.max), tag="s")

    def act(o, i, f=AF.Identity, bias=0.0, scale=1.0):
        rd = [i] + [s for s in (bias, scale) if isinstance(s, tuple)]
        bb = bias[0] if isinstance(bias, tuple) else bias
        ss = scale[0] if isinstance(scale, tuple) else scale
        add("a", max(64, o[4]) * CY + 40, rd, [o], lambda q: q.activation(o[0], i[0], f, bias=bb, scale=ss))

    def ag(o, win, off, bias=0.0):
        return add("a", 65 + o[4] * GA * CY, [win, off], [o],
                   lambda q: q.activation(o[0], win[0].indirect(off[0]), AF.Identity, bias=bias), tag="g")

    def mm(lst):
        cost = 0.0
        rd = {}
        for (o, l, r, st, sp) in lst:
            cost += max(min(64, l[4]), r[4]) * (4 if SB[l[1]][1] == F else 1) * PC
            for x in (l, r):
                rd[(x[1], x[2], x[3])] = x

        def fn(q):
            ins = None
            for (o, l, r, st, sp) in lst:
                ins = q.matmul(o[0], l[0], r[0], st, sp)
            return ins
        return add("p", cost + 20, list(rd.values()), [lst[0][0]], fn)

    def iota(o, pat, base, ch):
        if SB[o[1]][1] == I:
            fn = lambda q: q.iota(o[0], pat, base, ch)
        else:
            fn = lambda q: q.iota(o[0], pat, base, ch, allow_small_or_imprecise_dtypes=True)
        add("g", 130 + 2 * o[4] * CY, [], [o], fn)

    def dma(e, out, in_, rd, wr, lat):
        sem = T.sem[DMAS[nd[0]]]
        nd[0] += 1
        add(e, 60.0, rd, wr, lambda q: q.dma_start(out, in_).then_inc(sem, 16), kind="d", lat=lat, sem=sem, cnt=16)

    def send(dst_rank, src, land, name):
        dst = T.cores[dst_rank % n_r]
        rid, pid = topo.addr(dst, core)
        mask = topo.mask(core, dst)
        ne = len(topo.engines(core, dst))
        sent[0] += ne
        me = add("g", 900.0, [src], [], lambda q: q.remote_dma(land[0], src[0], T.sem[name], T.sem.sent, pid, rid, mask), kind="r")
        o = add("x", 0.0, [], [land], None, kind="x", lat=3200.0, sem=T.sem[name], cnt=ne)
        ops[o][4][me] = False

    dma("a", T.reci[:], T.rec[:], [], [A("reci")], 2000.0)
    first = len(ops)
    dma("s", T.Pi[:], T.par[:], [], [A("Pi")], 3500.0)
    dma("s", T.XZ[:, 0:R], T.prof[:], [], [A("XZ", 0, R)], 5000.0)
    soft.append((first, first + 1))
    dma("a", T.ZL[:, 0:L], T.zf[:], [], [A("ZL", 0, L)], 2500.0)
    dma("a", T.thi[:], T.th[:], [], [A("thi")], 2500.0)

    iota(A("pi", 0, 1), [[0, 1]], 0, 1)
    iota(A("ioC"), [[0, 6], [1, 16]], 0, 0)
    iota(A("ioB"), [[1, 128]], 0, 0)
    iota(A("ioA"), [[1, 32], [0, 16]], 0, 0)
    iota(A("DM"), [[96, 2], [0, 2], [16, 6]], V, 0)
    iota(A("ioD"), [[1, 8], [0, 17]], 0, 0)
    iota(A("ioE"), [[0, 8], [1, 17]], 0, 0)
    iota(A("ioF"), [[16, 8], [1, 17]], 0, 0)
    iota(A("xtab"), [[1, R + 4]], 0, 0)
    ts(A("pi", 1, 2), A("pi", 0, 1), 15, None, ALU.bitwise_and)
    ts(A("pi", 2, 3), A("pi", 0, 1), 4, None, ALU.arith_shift_right)
    ts(A("pi", 3, 4), A("pi", 0, 1), 31, None, ALU.bitwise_and)
    cp(A("pf", 0, 4), A("pi"))
    pc, kc, gc, p31 = A("pf", 0, 1), A("pf", 1, 2), A("pf", 2, 3), A("pf", 3, 4)
    ts(A("pf", 4, 5), pc, -8.0, None, ALU.add)
    ts(A("pf", 5, 6), kc, -4096.0, 16 * 4096.0 - MID, ALU.mult, ALU.add)
    ts(A("RM", 0, 96), A("ioC"), kc, None, ALU.is_equal)
    w0 = 96
    while w0 < 2576:
        n = min(w0, 2576 - w0)
        cp(A("RM", w0, w0 + n), A("RM", 0, n))
        w0 += n
    for h in range(2):
        ts(A("ND", 96 * h, 96 * h + 96), A("ioC"), kc, -float(2 ** 24), ALU.not_equal, ALU.mult)
    ts(A("BOf"), A("ioA", 0, 128), gc, None, ALU.is_equal)
    ts(A("If"), A("ioB"), pc, None, ALU.is_equal)
    ts(A("E"), A("ioA"), p31, None, ALU.is_equal)
    ms(A("RSn"), 0.0)
    ms(A("RSn", 0, 192, 16), -BIG)
    ms(A("RS17"), 0.0)
    ms(A("RS17", 0, 272, 17), BIG)
    ms(A("R01"), 1.0)
    ms(A("R01", 0, 128, 16), 0.0)
    ms(A("ones"), 1.0)
    act(A("I2", 0, 128), A("If"))
    act(A("I2", 128, 256), A("If"))
    act(A("nIf"), A("If"), scale=-1.0)
    act(A("nIb"), A("If"), scale=-1.0)
    act(A("penI"), A("If"), scale=-1024.0)
    act(A("brI"), A("If"), scale=121 * K16)
    act(A("nbI"), A("If"), scale=4096.0)
    act(A("TH", 256, 384), A("If"), scale=A("pf", 5, 6))
    act(A("Wo"), A("BOf"), scale=K16)
    G8 = A("BOf", 0, 128, 16)
    act(A("Wc", 0, 8), G8, scale=K16)
    act(A("Wc", 8, 16), G8, scale=K16)
    act(A("Wc", 16, 24), G8, scale=-2 * K16)
    wmade = {}

    def wts(a, b):
        if (a, b) not in wmade:
            j = 24 * len(wmade)
            if (-a, -b) in wmade:
                act(A("W", j, j + 24), wmade[(-a, -b)], scale=-1.0)
            else:
                for i, sc in enumerate((a, b, (a + b) * K16 / 2)):
                    act(A("W", j + 8 * i, j + 8 * i + 8), G8, scale=float(sc))
            wmade[(a, b)] = A("W", j, j + 24)
        return wmade[(a, b)]
    ms(A("crow", p=32), -240 * K16)
    ms(A("crow", 16, 272, 17, p=32), -MID)
    for h in range(2):
        act(A("crow", 136 * h, 136 * h + 136, p=1), A("ioE", p=1), bias=-MID, scale=4096.0)
    ts(A("I17"), A("ioF"), pc, None, ALU.is_equal)
    ms(A("I17", 16, 136, 17), 0.0)
    ms(A("crow", 16, 136, 17, p=1), -120 * K16)
    ms(A("crow", 152, 272, 17, p=1), float(2 ** 25))
    act(A("Q17"), A("I17"), scale=242 * K16)
    ts(A("B17"), A("ioD"), gc, K16, ALU.is_equal, ALU.mult)
    ms(A("B17", 16, 136, 17), 0.0)
    ms(A("pw", 0, 16), 0.5)
    ms(A("pw", 16, 32), 0.0)
    scan(A("pw", 32, 48), A("pw", 0, 16), A("pw", 16, 32), K16, ALU.mult, ALU.add)
    tt(A("pw", 0, 16), A("pw", 32, 48), A("RM", 0, 16), ALU.mult)
    total(A("pf", 6, 7), A("pw", 0, 16))
    ts(A("pf", 7, 8), A("pf", 6, 7), -8192.0, 4096.0, ALU.mult, ALU.add)
    act(A("Wd"), A("BOf"), scale=A("pf", 6, 7))
    ts(A("DM"), A("DM"), kc, None, ALU.add)
    ts(A("CL"), A("DM"), float(R - V), None, ALU.add)
    ts(A("DM"), A("DM"), C23, None, ALU.add)
    ts(A("ExY", p=16), A("ioA", 0, 128, p=16), A("pf", 0, 1, p=16), None, ALU.is_equal)
    ts(A("ExX", p=16), A("ioA", 0, 128, p=16), A("pf", 4, 5, p=16), None, ALU.is_equal)
    cp(A("thf"), A("thi"))
    ts(A("ngs", 0, 1), A("thf", 0, 1), -1.0, None, ALU.mult)
    for c in (1, 0):
        u0 = 32 * c
        cp(A("LU", u0, u0 + 6), A("reci", 6 * c, 6 * c + 6))
        ts(A("LU", u0 + 6, u0 + 12), A("reci", 6 * c, 6 * c + 6), 0.5, -0.25, ALU.mult, ALU.add)
    cp(A("Pf", 0, V), A("Pi"))
    X = A("XZ", 0, R)
    Ib = A("I2", 0, 128)

    def lanes(n, c, w=H, o=0, k=None):
        return A(n, c * w + o, c * w + (w if k is None else o + k))

    def red(out, c0, c1, step, data, c, wt, last=False):
        if data + str(c) in SPLIT:
            mm([(A(out, c0 + k, c1, step, p=64), A(data, c * 1536 + k, c * 1536 + 1024, 16), wt, False, False) for k in range(16)])
            mm([(A(out, c0 + k, c1, step, p=H, p0=64), A(data, c * 1536 + 1024 + k, (c + 1) * 1536, 16), wt, False, last and k == 15)
                for k in range(16)])
            return
        mm([(A(out, c0 + k, c1, step, p=H), A(data, c * 1536 + k, (c + 1) * 1536, 16), wt, False, last and k == 15) for k in range(16)])

    def piece(n, c, q):
        return A(n, c * 1536 + 512 * q, c * 1536 + 512 * q + 512)

    def prof(j, c, q):
        return (ag if GE[9 * c + 3 * j + q] == "a" else vg)(piece("W" + "ABC"[j], c, q), X, lanes("ABC"[j] + "u", c, H, 32 * q, 32))

    def dist(c, q, o, route, pairs, after):
        Eq = P("E", 32 * q, 32 * q + 32, 0, 512)
        rep = P("zpT", 32 * q, 32 * q + 32, 256 * c + o, 256 * c + o + 128)
        if route == "m":
            b = tile("r")
            soft.append((after, mm([(A(b), rep, Eq, True, True)])))
            for w, m in pairs:
                tt(piece(m, c, q), A(b), piece(w, c, q), ALU.min)
        else:
            for w, m in pairs:
                b = tile("r")
                mm([(A(b), rep, Eq, True, False), (A(b), A("nIb"), piece(w, c, q), False, True)])
                act(piece(m, c, q), A(b), AF.Abs)

    for t in range(RO):
        PW = A("Pi") if t == 0 else A("Pf", 0, V)
        lu = lambda c, j, n=1: A("LU", t * 64 + 32 * c + 6 * j, t * 64 + 32 * c + 6 * (j + n))
        zc = lambda c: A("ZL", t * L + H * c, t * L + H * c + H)
        xb = lambda c: lanes("xy", c, 2 * H, 0, H)
        yb = lambda c: lanes("xy", c, 2 * H, H, H)

        def column(j, c, off):
            n = "ABC"[j]
            if FA[j] == "1":
                ag(lanes(n + "f", c), A("Pf", 0, V), off)
            else:
                cp(lanes(n + "f", c), lanes(n + "u", c))

        def head(c):
            cur[0] = c
            act(A("XZ", R + H * c, R + H * c + H), zc(c))
            ag(lanes("rm", c), A("RM"), lu(c, 0))
            b = tile("m")
            mm([(A(b, 0, 128, p=H), zc(c), Ib, True, True)])
            act(A("zpT", 256 * c, 256 * c + 128, p=H), A(b, 0, 128, p=H))
            vg(lanes("Au", c), PW, lu(c, 1))
            vg(lanes("M", c), PW, lu(c, 1), lanes("rm", c), ALU.mult)
            b = tile("m")
            mm([(A(b, 0, H), A("BOf"), lanes("M", c), True, False), (A(b, 0, H), Ib, A("ND", 0, H), False, True)])
            scan(lanes("ys", c), A("RSn", 0, H), A(b, 0, H), 0.0, ALU.add, ALU.max)
            ysl = A("ys", H * c + 15, H * c + H, 16)
            ts(lu(c, 2), ysl, 0.5, -0.25, ALU.mult, ALU.add)
            cp(lu(c, 3), ysl)
            vg(lanes("Bu", c), PW, lu(c, 2))
            ag(lanes("p", c), X, lu(c, 3))
            b = tile("m")
            mm([(A(b, 0, 128, p=H), lanes("p", c), Ib, True, True), (A(b, 128, 128 + H), A("BOf"), lanes("M", c), True, True)])
            act(A("zpT", 256 * c + 128, 256 * c + 256, p=H), A(b, 0, 128, p=H))
            act(yb(c), A(b, 128, 128 + H))
            ag(xb(c), A("xtab"), lu(c, 0), -float(t))
            act(lanes("nrm", c), lanes("rm", c), bias=1.0, scale=-1.0)
            vg(lanes("Af", c), PW, lu(c, 1), lanes("nrm", c), ALU.mult)
            column(1, c, lu(c, 2))
            tt(lanes("eqab", c), lanes("Af", c), lanes("Bf", c), ALU.is_equal)
            act(lanes("gxy", c, 2 * H), lanes("xy", c, 2 * H), bias=C23, scale=0.4999)
            ts(A("gf", 16 * c, 16 * c + 12), lu(c, 1, 2), C23, None, ALU.add)

        def stage_ab(c):
            cur[0] = c
            rz, rp = RAB[c]
            KA = tile("k")
            for q in range(3):
                first = prof(0, c, q)
                prof(1, c, q)
                dist(c, q, 0, rz, (("WA", "MZA"), ("WB", "MZB")), first)
                dist(c, q, 128, rp, (("WA", "MPA"), ("WB", "MPB")), first)
            mm([(A(KA, 0, 384, p=H), A("ones", 0, H), A("TH"), True, False),
                (A(KA, 0, 128, p=H), lanes("rm", c), A("penI"), False, False),
                (A(KA, 0, 128, p=H), lanes("eqab", c), A("penI"), False, False),
                (A(KA, 256, 384, p=H), lanes("Bf", c), A("If"), False, False)])
            wa = (-1 if rz == "m" else 0, 1 if rp == "m" else 0)
            za = 2 if rz == "m" else -1
            pa = -2 if rp == "m" else 1
            if wa != (0, 0):
                red(KA, 0, 384, 16, "WA", c, wts(*wa))
                red(KA, 0, 384, 16, "WB", c, wts(-wa[0], -wa[1]))
            red(KA, 0, 384, 16, "MZA", c, wts(za, 0))
            red(KA, 0, 384, 16, "MZB", c, wts(-za, 0))
            red(KA, 0, 384, 16, "MPA", c, wts(0, pa))
            red(KA, 0, 384, 16, "MPB", c, wts(0, -pa), True)
            G0 = 256 * c
            w = A("w", 128 * c, 128 * c + 128, p=H)
            if WA_:
                ga, gm = A("ga", 128 * c, 128 * c + 128, p=H), A("gm", 128 * c, 128 * c + 128, p=H)
                act(ga, A(KA, 0, 128, p=H))
                tt(gm, A(KA, 128, 256, p=H), ga, ALU.min)
                act(w, gm, AF.Relu, bias=float(2 ** 25), scale=float(2 ** 25))
            else:
                act(A("G", G0, G0 + 256, p=H), A(KA, 0, 256, p=H), AF.Relu, bias=float(2 ** 25), scale=float(2 ** 25))
                tt(w, A("G", G0, G0 + 128, p=H), A("G", G0 + 128, G0 + 256, p=H), ALU.min)
            tt(A("key", 128 * c, 128 * c + 128, p=H), A(KA, 256, 384, p=H), w, ALU.min)

        def mid(c):
            cur[0] = c
            s = lambda n, w=128, o=0, k=None, st=1: A(n, w * c + o, w * c + (w if k is None else o + k), st, p=H)
            act(s("wit"), s("w"), AF.Sign)
            scan(s("ks"), A("RSn", 0, 128, p=H), s("key"), 0.0, ALU.add, ALU.max)
            scan(s("cs"), A("R01", p=H), s("wit"), 0.0, ALU.mult, ALU.add)
            act(s("nbL", 8), s("cs", 128, 15, None, 16), AF.Sign, bias=-2.5)
            kl = s("ks", 128, 15, None, 16)
            ts(s("kf", 8), kl, RND, -RND, ALU.add, ALU.add)
            b = tile("m")
            mm([(A(b, 0, H, p=8), kl, A("If", 0, H, p=H), True, False)])
            mm([(A(b, 0, H, p=8), s("kf", 8), A("nIf", 0, H, p=H), False, False),
                (A(b, 0, H, p=8), s("nbL", 8), A("nbI", 0, H, p=H), False, True)])
            act(A("vT", H * c, H * c + H, p=8), A(b, 0, H, p=8), bias=MID - 4096.0)
            b = tile("m")
            mm([(A(b, 0, H), A("ExY", p=8), A("vT", H * c, H * c + H, p=8), True, False), (A(b, 0, H), Ib, A("ND", 0, H), False, True)])
            scan(lanes("vs", c), A("RSn", 0, H), A(b, 0, H), 0.0, ALU.add, ALU.max)
            vl = A("vs", H * c + 15, H * c + H, 16)
            ts(lanes("gC", c, 8, 0, 6), vl, 0.5, -0.25, ALU.mult, ALU.add)
            vg(lanes("Cu", c), PW, lanes("gC", c, 8, 0, 6))
            column(2, c, lanes("gC", c, 8, 0, 6))
            tt(lanes("eqc", c, 2 * H, 0, H), lanes("Cf", c), yb(c), ALU.is_equal)
            tt(lanes("eqc", c, 2 * H, H, H), lanes("Cf", c), xb(c), ALU.is_equal)
            nb4 = lanes("nb4", c, 8, 0, 6)
            act(nb4, vl, AF.Relu, scale=-1.0)
            for r in range(2):
                tt(lanes("s", c, 16, 6 * r, 6), lanes("gf", c, 16, 6 * r, 6), nb4, ALU.add)
            tt(lanes("nbl", c, 8, 0, 6), nb4, A("CL", 12 * c, 12 * c + 6), ALU.min)

        def dedup(c):
            cur[0] = 0
            b = tile("m")
            lst = [(A(b, 0, 2 * H), Ib, A("ND"), True, False)]
            for r in range(2):
                e0 = (2 * c + r) * 6
                ee = lambda j, a, z: (T.EE[:, e0 + j, a:z], "EE", (e0 + j) * 112 + a, (e0 + j) * 112 + z, z - a)
                for j in range(6):
                    n = H - 16 * j
                    ts(ee(j, 0, n), lanes("gxy", c, 2 * H, r * H + 16 * j, n), lanes("s", c, 16, 6 * r + j, 1), None, ALU.is_equal)
                    if n > 16:
                        lst.append((A(b, r * H + 16 * j + 16, r * H + H), A("Wo"), ee(j, 16, n), False, False))
                lst.append((A(b, r * H, r * H + H), A("Wd"), (T.EE[:, e0:e0 + 6, 0:16], "EE", e0 * 112, (e0 + 6) * 112, H), False, r == 1))
            mm(lst)
            scan(lanes("ds", c, 2 * H), A("RSn"), A(b, 0, 2 * H), 0.0, ALU.add, ALU.max)
            q = lambda n: lanes(n, c, 16, 0, 12)
            act(q("t1"), A("ds", 2 * H * c + 15, 2 * H * (c + 1), 16), AF.Relu, bias=A("pf", 7, 8), scale=4096.0)
            tt(q("t2"), q("t1"), q("s"), ALU.add)
            tt(q("t3"), q("t2"), A("DM", 12 * c, 12 * c + 12), ALU.min)
            ts(q("off"), q("t3"), -C23, None, ALU.add)

        def count():
            b = tile("m")
            mm([(A(b, 0, 16), A("ones", p=H), A("nbL", p=H), True, True)])
            total(A("cn", 0, 1), A(b, 0, 16))
            ts(A("ci", 0, 1), A("cn", 0, 1), 0.5, 4.0 * L, ALU.mult, ALU.add)
            ts(A("ci", 1, 2), A("ci", 0, 1), 15, None, ALU.bitwise_and)
            ts(A("ngs", t + 1, t + 2), A("ci", 1, 2), A("thf", t + 1, t + 2), -1.0, ALU.add, ALU.mult)

        def stage_c(c):
            cur[0] = c
            rz, rp = RC[c]
            KC = tile("k")
            for q in range(3):
                first = prof(2, c, q)
                dist(c, q, 0, rz, (("WC", "MZC"),), first)
                dist(c, q, 128, rp, (("WC", "DPC"),), first)
            G1 = A("If", 0, 128, 16)
            lst = [(A(KC, 0, 272, p=H), A("ones", 0, H, p=2), A("crow", p=2), True, False),
                   (A(KC, 16, 136, 17, p=H), A("brI", 0, H, p=H), A("nbL", 8 * c, 8 * c + 8, p=H), False, False),
                   (A(KC, 16, 136, 17, p=H), yb(c), G1, False, False)]
            for o, route, own in ((0, rz, zc(c)), (136, rp, lanes("p", c))):
                if route == "m":
                    lst.append((A(KC, o, o + 136, p=H), own, A("B17"), False, False))
            mm(lst)
            for o in (0, 136):
                mm([(A(KC, o, o + 136, p=H), lanes("Cf", c), A("I17"), False, False)])
            if "m" in (rz, rp):
                red(KC, 0 if rz == "m" else 136, 272 if rp == "m" else 136, 17, "WC", c, A("Wc", 0, 16 if rz == rp else 8))
            red(KC, 0, 136, 17, "MZC", c, A("Wc", 16, 24) if rz == "m" else A("Wc", 0, 8))
            if rp == "m":
                red(KC, 136, 272, 17, "DPC", c, A("Wc", 16, 24))
            mm([(A(KC, 0, 136, p=H), lanes("eqc", c, 2 * H, 0, H), A("Q17"), False, False),
                (A(KC, 136, 272, p=H), lanes("eqc", c, 2 * H, H, H), A("Q17"), False, rp == "m")])
            if rp == "a":
                red(KC, 136, 272, 17, "DPC", c, A("Wc", 0, 8), True)
            scan(A("ks2", 272 * c, 272 * c + 272, p=H), A("RS17", p=H), A(KC, 0, 272, p=H), 0.0, ALU.add, ALU.min)

        def tail(c):
            cur[0] = c
            kl = A("ks2", 272 * c + 16, 272 * c + 272, 17, p=H)
            yf = A("yf", 16 * c, 16 * c + 16, p=H)
            ts(yf, kl, RND, -RND, ALU.add, ALU.add)
            b = tile("m")
            mm([(A(b, 0, H, p=16), kl, A("If", 0, H, p=H), True, False)])
            mm([(A(b, 0, H, p=16), yf, A("nIf", 0, H, p=H), False, True)])
            vT = A("vT2", H * c, H * c + H, p=16)
            act(vT, A(b, 0, H, p=16), bias=MID)
            b = tile("m")
            mm([(A(b, 0, H), A("nbI"), lanes("rm", c), True, False), (A(b, 0, H), A("ExY", p=16), vT, False, True)])
            act(lanes("Ym", c), A(b, 0, H), bias=-4096.0)
            vscat(A("Pf"), lanes("off", c, 16, 0, 6), lanes("Ym", c), lanes("Af", c))
            b = tile("m")
            mm([(A(b, 0, H), A("nbI"), lanes("rm", c), True, False), (A(b, 0, H), A("ExX", p=16), vT, False, True)])
            act(lanes("Xm", c), A(b, 0, H), bias=-4096.0)
            b = tile("m")
            mm([(A(b, H, 2 * H), Ib, A("ND", 0, H), True, False), (A(b, H, 2 * H), A("ExY", p=16), vT, False, True)])
            scan(lanes("xs", c), A("RSn", 0, H), A(b, H, 2 * H), 0.0, ALU.add, ALU.max)
            xl = A("xs", H * c + 15, H * c + H, 16)
            u0 = t * 64 + 32 * c
            if t + 1 < RO:
                ts(A("SU", u0, u0 + 6), xl, float(t + 1), None, ALU.add)
                ts(A("SU", u0 + 6, u0 + 12), xl, 0.5, -0.25, ALU.mult, ALU.add)
                send(rank + 1, A("SU", u0, u0 + 12), A("LU", u0 + 64, u0 + 76), "ax%d%d" % (t + 1, c))
            else:
                cp(A("XF", 8 * c, 8 * c + 6), xl)
                send(rank - t, A("XF", 8 * c, 8 * c + 6), A("XL", 8 * c, 8 * c + 6), "ax%d%d" % (t + 1, c))
            tt(lanes("wof", c, 8, 0, 6), xl, lanes("nbl", c, 8, 0, 6), ALU.max)
            cp(lanes("wou", c, 8, 0, 6), lanes("wof", c, 8, 0, 6))
            if ZA:
                ag(lanes("zw", c), A("XZ"), lanes("wou", c, 8, 0, 6))
                b = tile("m")
                mm([(A(b, 0, H), Ib, zc(c), True, False), (A(b, 0, H), Ib, lanes("zw", c), False, True)])
                act(lanes("zr", c), A(b, 0, H), bias=191.75, scale=0.5)
            else:
                vg(lanes("zs", c), A("XZ"), lanes("wou", c, 8, 0, 6), zc(c), ALU.add)
                act(lanes("zr", c), lanes("zs", c), bias=191.75, scale=0.5)
            z0 = t * L + H * c
            act(A("ZS", z0, z0 + H), lanes("zr", c), bias=-192.0)
            send(rank + 1 if t + 1 < RO else rank - t, A("ZS", z0, z0 + H), A("ZL", z0 + L, z0 + L + H), "az%d%d" % (t + 1, c))

        occ.clear()
        act(A("TH", 0, 256), A("I2"), scale=A("ngs", t, t + 1))
        head(1)
        head(0)
        stage_ab(1)
        mid(1)
        stage_ab(0)
        dedup(1)
        mid(0)
        if t + 1 < RO:
            count()
        dedup(0)
        stage_c(1)
        tail(1)
        stage_c(0)
        tail(0)
        for c in (1, 0):
            vg(lanes("B1", c), A("Pf", 0, V), lu(c, 2), lanes("nrm", c), ALU.mult)
        for c in (1, 0):
            vscat(A("Pf"), lanes("off", c, 16, 6, 6), lanes("Xm", c), lanes("B1", c))

    dma("s", T.ypar[:], T.Pf[:, 0:V], [A("Pf", 0, V)], [], 4000.0)
    for c in (1, 0):
        z0 = RO * L + H * c
        dma("s", T.yrec[:, 6 * c:6 * c + 6], T.XL[:, 8 * c:8 * c + 6], [A("XL", 8 * c, 8 * c + 6)], [], 2000.0)
        dma("a", T.yz[:, H * c:H * c + H], T.ZL[:, z0:z0 + H], [A("ZL", z0, z0 + H)], [], 2000.0)

    n = len(ops)
    succ = [[] for _ in range(n)]
    for i, o in enumerate(ops):
        for d in o[4]:
            succ[d].append(i)
    prio = [0.0] * n
    for i in range(n - 1, -1, -1):
        prio[i] = ops[i][1] + ops[i][2] + max([prio[j] + (HOP if ops[j][4][i] else 0.0) for j in succ[i]] + [0.0])
    extra = {}
    for w in PRI.split():
        k = max(w.rfind("+"), w.rfind("-"))
        extra[w[:k]] = 1000.0 * int(w[k:])
    prio = [prio[i] + BIAS * ops[i][9] + extra.get(ops[i][8][:-2][:2] + ops[i][8][-2], 0.0) for i in range(n)]
    left = [len(o[4]) for o in ops]
    softs = [[] for _ in range(n)]
    for a, b in soft:
        softs[a].append(b)
        left[b] += 1
    opens = {u[0]: nm for nm, u in users.items()}
    uses = [[] for _ in range(n)]
    for nm, u in users.items():
        for i in u:
            uses[i].append(nm)
    todo = {nm: len(u) for nm, u in users.items()}
    bank_of, holder, bfree, held = {}, [None] * 8, [0.0] * 8, {"r": 0, "k": 0, "m": 0}
    idle = list(range(8))
    tfin = {nm: 0.0 for nm in users}
    ready_t = [0.0] * n
    cand = [i for i in range(n) if left[i] == 0]
    free = {e: 0.0 for e in "vapgsx"}
    order = []
    tend = 0.0

    def start(i):
        s0 = max(ready_t[i], free[ops[i][0]])
        if i in opens:
            if not idle or held[opens[i][1]] >= CAP[opens[i][1]]:
                return 1e18
            s0 = max(s0, min(bfree[b] for b in idle))
        return s0
    while cand:
        best = min(cand, key=lambda i: (round(start(i) / GRAIN), -prio[i]))
        e = ops[best][0]
        st = start(best)
        assert st < 1e17
        cand.remove(best)
        order.append((best, st))
        if best in opens:
            nm = opens[best]
            b = min(idle, key=lambda x: bfree[x])
            idle.remove(b)
            held[nm[1]] += 1
            bank_of[nm] = b
            if holder[b] is not None:
                for u in users[holder[b]]:
                    if ops[u][0] != "p":
                        ops[best][4][u] = True
                        succ[u].append(best)
            holder[b] = nm
        if e != "x":
            free[e] = st + ops[best][1]
        fin = st + ops[best][1] + ops[best][2]
        tend = max(tend, fin)
        for nm in uses[best]:
            todo[nm] -= 1
            tfin[nm] = max(tfin[nm], fin + HOP)
            if todo[nm] == 0:
                idle.append(bank_of[nm])
                bfree[bank_of[nm]] = tfin[nm]
                held[nm[1]] -= 1
        for j in softs[best] + succ[best]:
            now = j in softs[best] or (ops[j][0] == e and not ops[j][4][best])
            ready_t[j] = max(ready_t[j], st if now else fin + HOP)
            left[j] -= 1
            if left[j] == 0:
                cand.append(j)
    for a in lazy:
        a[0] = T[BANKS[bank_of[a[1]]]][a[7]:a[6], a[2]:a[3]:a[5]] if a[5] > 1 else T[BANKS[bank_of[a[1]]]][a[7]:a[6], a[2]:a[3]]

    marked = [any(ops[j][4][i] for j in succ[i]) for i in range(n)]
    csem = {"v": T.sem.cv, "a": T.sem.ca, "p": T.sem.cp, "g": T.sem.cg}
    tick = {e: 0 for e in csem}
    stamp = [0] * n
    seen = {e: {} for e in Q}
    for i, st in order:
        e, cost, lat, fn, deps, kind, sem, cnt = ops[i][:8]
        if kind == "x":
            continue
        need = {}
        for d, w in deps.items():
            if w:
                key = ops[d][0] if ops[d][5] == "c" else d
                need[key] = max(need.get(key, 0), stamp[d] if ops[d][5] == "c" else ops[d][7])
        for key, val in need.items():
            if seen[e].get(key, 0) < val:
                Q[e].wait_ge(csem[key] if key in csem else ops[key][6], val)
                seen[e][key] = val
        ins = fn(Q[e])
        if kind == "c" and marked[i]:
            tick[e] += 1
            stamp[i] = tick[e]
            ins.then_inc(csem[e], 1)
    for e in csem:
        g.sync.wait_ge(csem[e], tick[e])
    for o in ops:
        if o[5] == "d":
            g.sync.wait_ge(o[6], o[7])
    g.wait_ge(T.sem.sent, sent[0])
    return (tend, order, ops)
